import numpy as np, ml_dtypes
CORES = [10,34,74,98]
N = 4
BF = ml_dtypes.bfloat16
def gentries(a):
    return np.ascontiguousarray(a.reshape(8, 16, -1).transpose(0, 2, 1)).reshape(8, -1)
def gtable(e):
    e = np.asarray(e); return np.ascontiguousarray(e.reshape(8, -1, 16).transpose(0, 2, 1)).reshape(128, -1).astype(np.int32)
W, P, S, V, Q, F = 4096, 256, 16, 6, 16, 4096
def parts(rng):
    return (rng.integers(0, 256, (N, 8, 16, W)), rng.integers(0, W, (N, 8, P, S)), rng.integers(0, W, (N, 8, P, S)), rng.integers(0, S + 1, (N, 8, P)),
            rng.integers(0, S + 1, (N, 8, P)), rng.integers(600, 1201, (N, 8, P)), rng.integers(0, 16, (N, 8, 16)))
def first(h, m):
    return np.where(m > 0, h[..., 0], (37 * np.arange(P)) & (F - 1))
def pack(x, h, t, m, n, th, w):
    return {"x0": np.ascontiguousarray(x.reshape(N, 128, W)).astype(np.float32).astype(BF), "hands": np.stack([gtable(a.reshape(8, -1)) for a in h]), "trains": np.stack([gtable(a.reshape(8, -1)) for a in t]),
            "mh": m.astype(np.int32), "nt": n.astype(np.int32), "th": th.astype(np.int32), "wt": np.ascontiguousarray(w.reshape(N, 128, 1)).astype(np.int32)}
def setup_inputs(rng):
    return pack(*parts(rng))
def setup_inputs_spread(rng):
    x, h, t, m, n, th, w = parts(rng)
    x = np.minimum((np.exp2(8 * rng.random((N, 8, 1, W))) * rng.random((N, 8, 16, W))).astype(np.int64), 255)
    h = np.minimum((W * rng.random(h.shape) ** 3).astype(np.int64), W - 1); t = W - 1 - np.minimum((W * rng.random(t.shape) ** 2).astype(np.int64), W - 1)
    m = np.minimum(((S + 1) * rng.random(m.shape) ** 2).astype(np.int64), S); n = S - np.minimum(((S + 1) * rng.random(n.shape) ** 2).astype(np.int64), S)
    th = np.minimum(np.exp2(12 * rng.random(th.shape)).astype(np.int64) - 1, 4080)
    return pack(x, h, t, m, n, th, w)
def setup_inputs_ends(rng):
    x, h, t, m, n, th, w = parts(rng); e = W - 1; q = N - 1
    x = 255 * rng.integers(0, 2, (N, 8, 16, W)); x = np.where(rng.random((N, 8, 1, W)) < 0.25, x[:, :, :1, :], x)
    for g, b in enumerate((0, 1, 2, 1, 0, 2, 1, 0)):
        if b < 2: x[:, g, :, 0] = 255 * b
    x[:, :, :, e] = 255 - x[:, :, :, 0]
    h = np.where(rng.random(h.shape) < 0.8, e * rng.integers(0, 2, h.shape), h); t = np.where(rng.random(t.shape) < 0.8, e * rng.integers(0, 2, t.shape), t)
    m = np.where(rng.random(m.shape) < 0.85, S * rng.integers(0, 2, m.shape), m); n = np.where(rng.random(n.shape) < 0.85, S * rng.integers(0, 2, n.shape), n)
    th = np.where(rng.random(th.shape) < 0.8, 4080 * rng.integers(0, 2, th.shape), np.maximum(255 * rng.integers(0, 17, th.shape) - rng.integers(0, 2, th.shape), 0))
    w = 15 * rng.integers(0, 2, w.shape); w[:, 0] = 15; w[:, 7] = 15; w[:, 3] = 0
    a = rng.integers(0, 2, (8, P - 8))
    h[q, :, 8:, 0] = e * a; t[q, :, 8:, 0] = e * a; t[q, :, 8:, 1:] = (e * (1 - a))[:, :, None]
    m[q, :, 8:] = S; n[q, :, 8:] = S; th[q, :, 8:] = 0
    th[q, :, 2] = 4080; n[q, :, 2] = S; m[q, :, 3] = 0; n[q, :, 3] = 0
    h[q, 7, P - 1, 0] = e; n[q, 7, P - 1] = 0
    h[q, 7, 1, 0] = e; t[q, 7, 1] = 0; m[q, 7, 1] = S; n[q, 7, 1] = S; th[q, 7, 1] = 0
    return pack(x, h, t, m, n, th, w)
def setup_inputs_corners(rng):
    x, h, t, m, n, th, w = parts(rng)
    kd = rng.integers(0, 10, (N, 8, P)); kd[:, :, :10] = np.arange(10); kd[:, :, P - 10:] = np.arange(10)
    kd[0] = rng.choice(np.array([1, 4, 6]), (8, P)); kd[1] = rng.choice(np.array([0, 2, 3]), (8, P))
    kd[0, 2, 5] = 5; kd[0, 7, P - 1] = 0
    m = np.array([0, 0, S, S, 1, 1, S, 2, S - 1, 3])[kd]; n = np.array([0, S, 0, S, S, S - 1, S, S, S, 1])[kd]
    c = np.where(m > 0, h[..., 0], (37 * np.arange(P)) & (F - 1))
    t = (c[..., None] + rng.integers(1, W, t.shape)) % W; s = np.arange(S); k = kd[..., None]
    own = (((k == 1) | (k == 4) | (k == 5) | (k == 6)) & (s == 0)) | ((k == 7) & (s == S - 1)) | ((k == 8) & ((s == 3) | (s == 5))) | (k == 9)
    t = np.where(own, c[..., None], t)
    th = np.where((kd == 0) | (kd == 2), rng.choice(np.array([0, 1, 4079, 4080]), th.shape), 0)
    w[:, 1] = 0; w[:, 3] = 15; w[:, 5] = 0; w[:, 5, 15] = 1; w[:, 6] = 0; w[:, 6, 0] = 15
    return pack(x, h, t, m, n, th, w)
def setup_inputs_ties(rng):
    x, h, t, m, n, th, w = parts(rng)
    x = 4 * rng.integers(0, 64, (N, 8, 1, W)) + np.zeros((1, 1, 16, 1), np.int64)
    x[:, ::2] = x[:, ::2] + rng.integers(0, 2, (N, 4, 16, W)) * (rng.random((N, 4, 1, W)) < 0.25)
    th = np.maximum(64 * rng.integers(0, 12, th.shape) + rng.integers(-1, 2, th.shape), 0)
    t[:, 1::2] = np.where(rng.random((N, 4, P, S)) < 0.15, h[:, 1::2, :, :1], t[:, 1::2])
    t[:, 2] = rng.choice(np.array([0, 1, W - 2, W - 1]), (N, P, S)); h[:, 4] = rng.choice(np.array([0, 7, W - 1]), (N, P, S)); t[:, 6] = t[:, 6, :, :1]
    a = np.maximum(n[1], 1).reshape(-1); a[rng.permutation(8 * P)[:256]] = 0; n[1] = a.reshape(8, P)
    t[1] = np.where(np.arange(S) == n[1][..., None] - 1, first(h[1], m[1])[..., None], t[1])
    return pack(x, h, t, m, n, th, w)
def setup_inputs_counts(rng):
    x, h, t, m, n, th, w = parts(rng); b = N - 1; D = min(N - 3, V - 2, 3); p = b - D; s = np.arange(S)
    x[:2, 7] = np.where(np.arange(W) % 2 == 0, rng.integers(250, 256, (2, 16, W)), rng.integers(0, 10, (2, 16, W))); w[0, 7] = 15
    m[0, 1] = 0; n[0] = S
    m[1, 2] = 0; n[1] = np.maximum(n[1], 1); n[1, 2] = 0; n[1, 3, rng.permutation(P)[:99]] = 0
    c = first(h, m)
    t[:2] = (c[:2, ..., None] + 1 + 2 * rng.integers(0, W // 2, (2, 8, P, S))) % W
    t[0, ..., 0] = c[0]
    t[1, :7] = np.where(s == n[1, :7, :, None] - 1, c[1, :7, :, None], t[1, :7])
    XT = np.take_along_axis(x[:2], t[:2].reshape(2, 8, 1, P * S), 3).reshape(2, 8, 16, P, S); XC = np.take_along_axis(x[:2], c[:2, :, None, :], 3)
    d = np.add.reduce(np.abs(XT - XC[..., None]), axis=2)
    th[0] = np.maximum(np.min(d[0, ..., 1:], axis=-1) - 1, 0)
    th[1, 7] = np.take_along_axis(d[1, 7], n[1, 7][:, None] - 1, 1)[:, 0]
    th[p:] = 0; n[p:] = np.maximum(n[p:], 1); n[p] = S - D
    t[p:] = 8 * rng.integers(0, W // 8, (N - p, 8, P, S)); t[p, ..., 1:] = (t[p, ..., :1] + 8 * rng.integers(1, W // 8, (8, P, S - 1))) % W
    t[p:, :, P - 2:] = t[p:, :, P - 2:] + 4
    for u in range(D):
        h[p + u] = 8 * rng.integers(0, W // 8, (8, P, S)) + 1 + u; m[p + u] = rng.integers(D, S + 1, (8, P))
    h[b] = 8 * rng.integers(0, W // 8, (8, P, S)) + 7; h[b, ..., D] = np.roll(t[p, ..., 0], D, axis=0)
    m[b] = rng.integers(D + 1, S + 1, (8, P)); m[b, :, P - 2:] = 0
    return pack(x, h, t, m, n, th, w)
def check_inputs(d):
    bad = []
    for k, lo, hi in (("x0", 0, 255), ("hands", 0, W - 1), ("trains", 0, W - 1), ("mh", 0, S), ("nt", 0, S), ("th", 0, 4080), ("wt", 0, 15)):
        v = np.asarray(d[k]).astype(np.float64)
        if not (np.min(v) >= lo and np.max(v) <= hi): bad.append("range of " + k)
        elif np.any(v != np.rint(v)): bad.append("whole numbers of " + k)
    return bad
def reference(x0, hands, trains, mh, nt, th, wt):
    X = x0.astype(np.float32).astype(np.int32).reshape(N, 8, 16, W); s = np.arange(S); i = np.arange(P)
    H = np.stack([gentries(a) for a in hands]).astype(np.int64).reshape(N, 8, P, S); T = np.stack([gentries(a) for a in trains]).astype(np.int64).reshape(N, 8, P, S)
    m = mh.astype(np.int64); n = nt.astype(np.int64); lim = th.astype(np.int64); wv = wt.astype(np.int64).reshape(N, 8, 16, 1)
    H = np.where(s < m[..., None], H, 0); T = np.where(s < n[..., None], T, 0)
    A = np.zeros(N, np.int64); zero = np.zeros((N, 8, P, 1), np.int64)
    for t in range(V):
        if t > 0:
            j = 1 + t // N - (t - 1) // N
            T = np.roll(T, (1, j), axis=(0, 1)); n = np.roll(n, (1, j), axis=(0, 1))
        A3 = A[:, None, None]
        c = np.where(m > 0, H[..., 0], (37 * i + 613 * t + A3) & (F - 1))
        H = np.concatenate([H[..., 1:], zero], axis=-1); m = np.maximum(m - 1, 0)
        XT = np.take_along_axis(X, T.reshape(N, 8, 1, P * S), 3).reshape(N, 8, 16, P, S); XC = np.take_along_axis(X, c[:, :, None, :], 3)
        dist = np.add.reduce(np.abs(XT - XC[..., None]), axis=2)
        ok = (dist <= (lim + (A3 & 255))[..., None]) & (s < n[..., None])
        k = np.max(np.where(ok, s, -1), axis=-1); hit = k >= 0; got = np.where(hit, n - k, 0)
        XS = np.take_along_axis(XT, np.maximum(k, 0)[:, :, None, :, None], 4)[..., 0]
        y = np.where(hit[:, :, None, :], (XC + XS) >> 1, np.where((n == 0)[:, :, None, :], XC, np.abs(XC - XS)))
        z = np.add.reduce(wv * y, axis=2) & (Q - 1)
        np.put_along_axis(X, (Q * i + z)[:, :, None, :], y, 3)
        h1 = hit[..., None]; m1 = m[..., None]; c1 = c[..., None]; n1 = n[..., None]
        back = np.take_along_axis(T, np.clip(m1 + n1 - s, 0, S - 1), 3)
        H = np.where(h1 & (s == m1), c1, np.where(h1 & (s > m1) & (s <= m1 + got[..., None]), back, H))
        m = np.where(hit, np.minimum(m + 1 + got, S), m)
        grown = np.where(n1 == S, np.concatenate([T[..., 1:], zero], axis=-1), T)
        grown = np.where(s == np.minimum(n1, S - 1), c1, grown)
        T = np.where(h1, np.where(s < k[..., None], T, 0), grown); n = np.where(hit, k, np.minimum(n + 1, S))
        A = np.sum(got, axis=(1, 2))
    return {"yx": X.reshape(N, 128, W).astype(np.float32).astype(BF), "yh": np.stack([gtable(a.reshape(8, -1)) for a in H]).astype(np.float32), "yt": np.stack([gtable(a.reshape(8, -1)) for a in T]).astype(np.float32),
            "ym": m.astype(np.float32), "yn": n.astype(np.float32)}

@@ -1,0 +1,587 @@
+import numpy as np
+from concourse.mybir import AluOpType, AxisListType, ActivationFunctionType
+
+V = 6
+SCRATCH = {}
+
+
+def _sb(names, shape, dtype, where="sbuf"):
+    for nm in names.split():
+        SCRATCH[nm] = (where, shape, dtype)
+
+
+_CF = ("m m1 q cf na d nm1 n kc t1 t2 t3 t4 kz k g0 n16 b0 z3 p0 IC IC37 IC16 KCB DN DD ROW RM").split()
+_CI = "fi fj z1 z2 e1 e2".split()
+_CU = "CL ZL SL EL BL".split()
+_MB = "IDB NIB SCI PENI GM REV ROTD REVD AI LGD ONB GR1 GR2 GRR1 GRR2 ZZB R6A R6B ROTN".split()
+_sb("X", [128, 4096], "bfloat16")
+_sb("XW", [128, 4624], "bfloat16")
+_sb("AB", [128, 16, 16, 18], "bfloat16")
+_sb("XC D0B A0B YB OH", [128, 256], "bfloat16")
+_sb("XC2", [128, 16, 16, 2], "bfloat16")
+_sb("XCB OHD L1 UF HF YTF TSB YH YT", [128, 256], "float32")
+_sb("Y2 XS XL HM T5B", [128, 256], "float16")
+_sb("TO16", [128, 272], "float16")
+_sb("DEAD", [128, 16, 18], "bfloat16")
+_sb("SCN", [128, 16, 16], "float32")
+_sb("H HX TR MTI", [128, 256], "int32")
+_sb("W", [128, 4096], "float32")
+_sb("D3", [8, 32, 256], "float32", "dram")
+_sb("THH THL ONE", [128, 288], "bfloat16")
+_sb("VC R", [128, 288], "float32")
+_sb("MB", [128, 128 * len(_MB)], "bfloat16")
+_sb("ID32 REV32 ROT6 ONF", [128, 128], "float32")
+_sb("TIND TINM TW TBC", [128, 16, 128], "bfloat16")
+_sb("ZO", [128, 512], "bfloat16")
+_sb("PI PMI WTI AINT AIN2", [128, 1], "int32")
+_sb("PM WF ACOL AF PM16", [128, 1], "float32")
+_sb("CF", [128, len(_CF), 16], "float32")
+_sb("CI", [128, len(_CI), 16], "int32")
+_sb("CU", [128, 16 * len(_CU)], "uint16")
+_sb("LGI LGJ", [128, 8], "int32")
+_sb("LGF LGS", [128, 8], "float32")
+_sb("MT", [128, 768], "int32")
+_sb("MTB", [128, 1024], "bfloat16")
+_sb("CP", [128, 4, 16], "bfloat16")
+_sb("c16", [128, 16], "float16")
+_sb("GOT", [128, 16], "bfloat16")
+_sb("PK1 PK2", [128, 32], "bfloat16")
+_sb("LT", [128, 272 * V], "uint16")
+_sb("SD", [128, 272 * V], "uint16")
+_sb("OC OU OS", [128, 3 * V, 16], "bfloat16")
+_sb("YM", [128, 512], "float32")
+_sb("D0 D1", [128, 4, 16, 16], "float32", "psum")
+_sb("E", [128, 288], "float32", "psum")
+_sb("GB TB", [128, 512], "float32", "psum")
+_sb("SM", [128, 32, 16], "float32", "psum")
+
+SEMAPHORES = (["sv", "ss", "sp", "sg", "ls", "lx0", "lx1", "lh", "lt", "lm", "lw", "ox", "ox2", "oh", "oy", "om"]
+              + ["hw%d" % t for t in range(V)] + ["hr%d" % t for t in range(V)]
+              + ["al%d" % t for t in range(1, V)] + ["ao%d" % t for t in range(1, V)])
+PS = {"pD0", "pD1", "pE", "pGB", "pTB", "pSM"}
+
+
+def rank_program(g, core, T, topo):
+    rank = T.rank_of(core)
+    if rank is None:
+        return
+    A = AluOpType
+    ACT = ActivationFunctionType
+    nxt = T.cores[(rank + 1) % len(T.cores)]
+    neng = len(topo.engines(core, nxt))
+    eng = {"v": g.vector, "s": g.scalar, "p": g.tensor, "g": g, "y": g.sync}
+    own = {"v": "sv", "s": "ss", "p": "sp", "g": "sg"}
+    cnt, tok, lastw, acc = {}, {}, {}, {}
+    clk = {q: {} for q in eng}
+
+    def need(q, R, W):
+        nd = {}
+
+        def add(t, mine):
+            if t is None or (t[0] == own.get(q) and (q == "p" or not mine)):
+                return
+            if clk[q].get(t[0], 0) < t[1]:
+                nd[t[0]] = max(nd.get(t[0], 0), t[1])
+        for k in R:
+            add(lastw.get(k), True)
+            if k in PS:
+                for t in acc.get(k, {}).items():
+                    add(t, False)
+        for k in W:
+            add(lastw.get(k), True)
+            for t in acc.get(k, {}).items():
+                add(t, True)
+        items = sorted(nd.items())
+        for s, v in items:
+            if clk[q].get(s, 0) >= v or any(tok.get(o, {}).get(s, 0) >= v for o in items if o[0] != s):
+                continue
+            eng[q].wait_ge(T.sem[s], v)
+            clk[q][s] = v
+            for s2, v2 in tok.get((s, v), {}).items():
+                if clk[q].get(s2, 0) < v2:
+                    clk[q][s2] = v2
+
+    def done(q, s, v, R, W):
+        tok[(s, v)] = dict(clk[q])
+        for k in R:
+            acc.setdefault(k, {})[s] = v
+        for k in W:
+            lastw[k] = (s, v)
+            acc[k] = {s: v} if k in PS else {}
+
+    def op(q, fns, R, W):
+        R, W = R.split(), W.split()
+        need(q, R, W)
+        s = own[q]
+        for f in (fns if isinstance(fns, list) else [fns]):
+            f().then_inc(T.sem[s], 1)
+            cnt[s] = cnt.get(s, 0) + 1
+        done(q, s, cnt[s], R, W)
+
+    def dma(q, pairs, R, W, s):
+        R, W = R.split(), W.split()
+        need(q, R, W)
+        for o, i in pairs:
+            eng[q].dma_start(o, i).then_inc(T.sem[s], 16)
+            cnt[s] = cnt.get(s, 0) + 16
+        done(q, s, cnt[s], R, W)
+
+    def arrive(s, k):
+        cnt[s] = neng
+        tok[(s, neng)] = {}
+        lastw[k] = (s, neng)
+
+    def tt(o, a, b, f, R, W):
+        op("v", lambda: g.vector.tensor_tensor(o, a, b, f), R, W)
+
+    def ts(o, a, s1, f1, s2, f2, R, W):
+        if f2 is None:
+            op("v", lambda: g.vector.tensor_scalar(o, a, s1, None, f1), R, W)
+        else:
+            op("v", lambda: g.vector.tensor_scalar(o, a, s1, s2, f1, f2), R, W)
+
+    def cp(o, a, R, W):
+        op("v", lambda: g.vector.tensor_copy(o, a), R, W)
+
+    def act(o, a, f, R, W, bias=0.0, scale=1.0):
+        op("s", lambda: g.scalar.activation(o, a, f, bias=bias, scale=scale), R, W)
+
+    def mm(o, l, r, st, sp):
+        return lambda: g.tensor.matmul(o, l, r, st, sp)
+
+    def pe(ms, R, W):
+        op("p", ms, R, W)
+
+    def fill(ap, c, W):
+        op("v", lambda: g.vector.memset(ap, c), "", W)
+
+    def remote(dst, src, rs, key):
+        need("g", [key], [])
+        rid, pid, _ = topo.addr(nxt)
+        g.remote_dma(dst, src, T.sem[rs], T.sem["ls"], pid, rid, topo.mask(core, nxt))
+        cnt["ls"] = cnt.get("ls", 0) + neng
+
+    def C(n):
+        return T.CF[:, _CF.index(n), :]
+
+    def I(n):
+        return T.CI[:, _CI.index(n), :]
+
+    def U(n):
+        return T.CU[:, 16 * _CU.index(n):16 * _CU.index(n) + 16]
+
+    def M(n, a=0, b=128, step=1):
+        k = 128 * _MB.index(n)
+        return T.MB[:, k + a:k + b:step]
+
+    ID, NI = M("IDB"), M("NIB")
+    XALL = "X Xh"
+
+    dma("s", [(T.TR[:], T.trains[:])], "", "TR", "lt")
+    dma("y", [(T.H[:], T.hands[:])], "", "H", "lh")
+    fill(T.MT[:], 0, "MT")
+    dma("s", [(T.X[:, 0:2048], T.x0[:, 0:2048])], "", "X", "lx0")
+    dma("y", [(T.MT[0:128:16, 0:256], T.mh[:]), (T.MT[0:128:16, 256:512], T.nt[:]), (T.MT[0:128:16, 512:768], T.th[:])],
+        "", "MT", "lm")
+    dma("y", [(T.X[:, 2048:4096], T.x0[:, 2048:4096])], "", "Xh", "lx1")
+    dma("y", [(T.WTI[:], T.wt[:])], "", "WTI", "lw")
+    fill(M("ONB"), 1.0, "ONB")
+    fill(T.ONF[:], 1.0, "ONF")
+    fill(T.TIND[:], 0.0, "TIND")
+
+    def iota(o, pat, base, cm, W, fl):
+        if fl:
+            op("g", lambda: g.iota(o, pat, base, cm, allow_small_or_imprecise_dtypes=True), "", W)
+        else:
+            op("g", lambda: g.iota(o, pat, base, cm), "", W)
+
+    def pick(o, i, pat, c, b, m, R, W):
+        op("g", lambda: g.affine_select(o, i, pat, c, 0.0, b, m), R, W)
+    iota(T.PI[:], [[0, 1]], 0, 1, "PI", False)
+    iota(C("ROW"), [[1, 16]], 0, 0, "ROW", True)
+    pick(M("ZZB"), M("ONB"), [[-16, 8], [0, 16]], A.is_ge, 0, 1, "ONB", "ZZB")
+    pick(M("GM"), M("ZZB"), [[16, 8], [0, 16]], A.is_ge, 15, -1, "ZZB", "GM")
+    pick(ID, M("ONB"), [[-1, 128]], A.is_equal, 0, 1, "ONB", "IDB")
+    iota(T.VC[:], [[256, 16], [1, 18]], 255, 0, "VC", True)
+    iota(T.SCN[:], [[0, 16], [1, 16]], 0, 0, "SCN", True)
+    iota(T.LGI[:], [[-1, 8]], 15, 1, "LGI", False)
+    pick(M("REV"), M("ONB"), [[-16, 8], [1, 16]], A.is_equal, -15, 1, "ONB", "REV")
+    pick(T.REV32[:], T.ONF[:], [[-16, 8], [1, 16]], A.is_equal, -15, 1, "ONF", "REV32")
+    pick(T.ID32[:], T.ONF[:], [[-1, 128]], A.is_equal, 0, 1, "ONF", "ID32")
+    pick(M("ROTD"), M("GM"), [[-16, 8], [-1, 16]], A.is_equal, -1, 1, "GM", "ROTD")
+    pick(M("ZZB"), M("GM"), [[-16, 8], [-31, 16]], A.is_equal, 465, 1, "GM", "ZZB")
+    pick(M("R6A"), M("GM"), [[-16, 8], [-1, 16]], A.is_equal, -6, 1, "GM", "R6A")
+    pick(M("R6B"), M("GM"), [[-16, 8], [-1, 16]], A.is_equal, 10, 1, "GM", "R6B")
+    pick(M("REVD"), M("GM"), [[-16, 8], [1, 16]], A.is_equal, -16, 1, "GM", "REVD")
+
+    ts(T.PMI[:], T.PI[:], 15, A.bitwise_and, None, None, "PI", "PMI")
+    cp(T.PM[:], T.PMI[:], "PMI", "PM")
+    ts(C("RM"), C("ROW"), T.PM[:], A.is_equal, None, None, "ROW PM", "RM")
+    ts(C("IC"), C("ROW"), 16.0, A.mult, T.PM[:], A.add, "ROW PM", "IC")
+    RM = lambda k: T.CF[:, _CF.index("RM"), k:k + 1]
+    op("v", [(lambda r=r: g.vector.tensor_copy(T.TIND[:, r, r:128:16], M("GM", r, 128, 16))) for r in range(16)], "GM TIND", "TIND")
+    cp(T.LT[:, 0:256], T.TR[:], "TR", "LT0")
+    ts(T.HM[:], T.H[:], -2048.0, A.add, RM(0), A.mult, "H RM", "HM")
+    cp(T.MTB[:, 0:512], T.MT[:, 0:512], "MT", "MTB")
+    ts(T.MTI[:], T.MT[:, 512:768], 4, A.arith_shift_right, None, None, "MT", "MTI")
+    cp(T.MTB[:, 512:768], T.MTI[:], "MTI", "MTB")
+    ts(T.MTI[:], T.MT[:, 512:768], 15, A.bitwise_and, None, None, "MT", "MTI")
+    cp(T.MTB[:, 768:1024], T.MTI[:], "MTI", "MTB")
+    pe([mm(T.SM[:, 20, :], T.TIND[:, r, :], T.HM[:, r:256:16], r == 0, r == 15) for r in range(16)], "TIND HM", "pSM")
+    ts(C("q"), T.SM[:, 20, :], 2048.0, A.add, None, None, "pSM", "q")
+    pe([mm(T.SM[:, 16:20, :], T.TIND[:, r, :], T.MTB[:, r:1024:16], r == 0, r == 15) for r in range(16)], "TIND MTB", "pSM")
+    cp(T.CP[:], T.SM[:, 16:20, :], "pSM", "CP")
+    cp(C("m"), T.CP[:, 0, :], "CP", "m")
+    ts(C("na"), C("m"), 0.0, A.is_le, None, None, "m", "na")
+    ts(C("IC37"), C("IC"), 37.0, A.mult, None, None, "IC", "IC37")
+    cp(I("fi"), C("IC37"), "IC37", "fi")
+    ts(I("fj"), I("fi"), 4095, A.bitwise_and, None, None, "fi", "fj")
+
+    def c_tail():
+        tt(C("d"), I("fj"), C("q"), A.subtract, "fj q", "d")
+        tt(C("d"), C("d"), C("na"), A.mult, "d na", "d")
+        tt(C("cf"), C("q"), C("d"), A.add, "q d", "cf")
+        cp(U("CL"), C("cf"), "cf", "CL")
+
+    def c_post():
+        ts(T.c16[:], C("cf"), -2048.0, A.add, None, None, "cf", "c16")
+        ts(C("m1"), C("m"), -1.0, A.add, 0.0, A.max, "m", "m1")
+        ts(C("p0"), C("m1"), 0.0, A.is_le, None, None, "m1", "p0")
+
+    def setup_a():
+        cp(T.OC[:, 0, :], T.CP[:, 1, :], "CP", "OC0")
+        fill(T.OC[:, 1, :], 0.0, "OC0")
+        fill(T.OC[:, 2, :], 1.0, "OC0")
+        ts(T.CP[:, 3, :], T.CP[:, 3, :], 1.0, A.add, None, None, "CP", "CP")
+        ts(NI, ID, -1.0, A.mult, None, None, "IDB", "NIB")
+        ts(M("SCI"), ID, 8192.0, A.mult, None, None, "IDB", "SCI")
+        ts(M("PENI"), ID, -134217728.0, A.mult, None, None, "IDB", "PENI")
+
+    def setup_b():
+        ts(T.TINM[:], T.TIND[:], -8192.0, A.mult, None, None, "TIND", "TINM")
+        ts(T.XS[:], T.TR[:], -2048.0, A.add, None, None, "TR", "XS")
+        fill(T.XW[:, 4352:4624], 0.0, "XWc XWz")
+        fill(T.AB[:, :, :, 0], 0.0, "ABz")
+        fill(T.AB[:, :, :, 17], 0.0, "ABc")
+        for nm, j, src in (("GR1", 1, "IDB"), ("GR2", 2, "IDB")):
+            cp(M(nm, 16 * j, 128), M(src, 0, 128 - 16 * j), src, nm)
+            cp(M(nm, 0, 16 * j), M(src, 128 - 16 * j, 128), src, nm)
+        ts(C("IC16"), C("IC"), 16.0, A.mult, None, None, "IC", "IC16")
+        ts(C("KCB"), C("IC16"), 256.0, A.add, None, None, "IC16", "KCB")
+        ts(C("DD"), C("IC"), -1.0, A.mult, 256.0, A.add, "IC", "DD")
+        ts(C("DN"), C("IC"), -15.0, A.mult, 4096.0, A.add, "IC", "DN")
+        ts(T.PM16[:], T.PM[:], 16.0, A.mult, None, None, "PM", "PM16")
+        ts(T.VC[:], T.VC[:], T.PM16[:], A.add, None, None, "VC PM16", "VC")
+        cp(T.VC[:, 0:288:18], C("IC"), "IC", "VC")
+        ts(T.VC[:, 17:288:18], C("IC"), 4352.0, A.add, None, None, "IC", "VC")
+        fill(T.DEAD[:], 0.0, "DEAD")
+
+    def setup_c():
+        cp(T.WF[:], T.WTI[:], "WTI", "WF")
+        ts(T.WF[:], T.WF[:], 0.5, A.mult, None, None, "WF", "WF")
+        ts(T.TW[:], T.TIND[:], T.WF[:], A.mult, None, None, "TIND WF", "TW")
+        ts(T.LGJ[:], T.LGI[:], 15, A.bitwise_and, None, None, "LGI", "LGJ")
+        cp(T.LGF[:], T.LGJ[:], "LGJ", "LGF")
+        ts(T.LGS[:], T.LGF[:], -8192.0, A.mult, -4096.0, A.add, "LGF", "LGS")
+        fill(T.ZO[:, 0:256], 0.0, "ZO")
+        fill(T.ZO[:, 256:512], 1.0, "ZO")
+        op("v", [(lambda r=r: g.vector.tensor_scalar(T.TBC[:, r, :], M("GM"), RM(r), None, A.mult)) for r in range(16)],
+           "GM RM", "TBC")
+
+    def setup_d():
+        tt(M("ROTD"), M("ROTD"), M("ZZB"), A.add, "ROTD ZZB", "ROTD")
+        tt(M("ROTD"), M("ROTD"), ID, A.subtract, "ROTD IDB", "ROTD")
+        pick(M("ZZB"), M("GM"), [[-16, 8], [31, 16]], A.is_equal, 0, 1, "GM", "ZZB")
+        ts(M("ROTN"), M("ROTD"), -1.0, A.mult, None, None, "ROTD", "ROTN")
+        for nm, j, src in (("GRR1", 1, "ROTD"), ("GRR2", 2, "ROTD")):
+            cp(M(nm, 16 * j, 128), M(src, 0, 128 - 16 * j), src, nm)
+            cp(M(nm, 0, 16 * j), M(src, 128 - 16 * j, 128), src, nm)
+        fill(T.ONE[:], 1.0, "ONE")
+        tt(M("REVD"), M("REVD"), M("ZZB"), A.add, "REVD ZZB", "REVD")
+        tt(M("REVD"), M("REVD"), M("REV"), A.subtract, "REVD REV", "REVD")
+        tt(T.ROT6[:], M("R6A"), M("R6B"), A.add, "R6A R6B", "ROT6")
+
+    def thresholds():
+        pe([mm(T.E[:, k:288:18], ID, T.CP[:, 2, :], True, True) for k in range(18)], "IDB CP", "pE")
+        act(T.THH[:], T.E[:], ACT.Identity, "pE", "THH", scale=16.0)
+        pe([mm(T.E[:, k:288:18], ID, T.CP[:, 3, :], True, True) for k in range(18)], "IDB CP", "pE")
+        act(T.THL[:], T.E[:], ACT.Identity, "pE", "THL")
+        fill(T.THH[:, 0:288:18], 4080.0, "THH")
+
+    XWK = "XW0 XW1 XW2 XW3 XW4"
+    PIECE = {0: (0, 64), 1: (64, 128), 2: (128, 192), 3: (192, 224), 4: (224, 256)}
+
+    def gather(q, t, b):
+        lo, hi = PIECE[b]
+        w = T.X[:].indirect(T.LT[:, 272 * t + lo:272 * t + hi])
+        o = T.XW[:, 256 + 16 * lo:256 + 16 * hi]
+        if q == "s":
+            act(o, w, ACT.Identity, XALL + " LT%d" % t, "XW%d" % b)
+        else:
+            cp(o, w, XALL + " LT%d" % t, "XW%d" % b)
+
+    def diff(b):
+        D = T["D%d" % (b % 2)]
+        ms = []
+        for h in range(2):
+            ms.append(mm(D[:, 2 * h:2 * h + 2, :, :], ID, T.XW[:, 256 + 1024 * b + 512 * h:768 + 1024 * b + 512 * h], True, False))
+            for s in range(8):
+                ms.append(mm(D[:, 2 * h:2 * h + 2, :, 2 * s:2 * s + 2], NI,
+                             T.XC2[:, 4 * b + 2 * h:4 * b + 2 * h + 2, :, :], False, s == 7))
+        pe(ms, "IDB NIB XC2 XW%d" % b + (" XW4" if b == 3 else ""), "pD%d" % (b % 2))
+
+    def absd(b):
+        act(T.AB[:, 4 * b:4 * b + 4, :, 1:17], T["D%d" % (b % 2)][:], ACT.Abs, "pD%d" % (b % 2), "AB%d" % b)
+
+    def dsum(b, last=False):
+        pe([mm(T.E[:, 72 * b:72 * b + 72], T.TINM[:, r, :], T.AB[:, 4 * b:4 * b + 4, r, :], False, last and r == 15)
+            for r in range(16)], "TINM ABz ABc AB%d" % b, "pE")
+
+    def spread(dst, wid, src, first, last=True):
+        return [mm(dst[:, r:wid:16], T.TBC[:, r, :], src, first, first or (last and r == 15)) for r in range(16)]
+
+    def oc(b, t, k):
+        return T[b][:, 3 * t + k, :]
+
+    def norm_compact(b, t, key):
+        cp(T.PK1[:, 0:16], oc(b, t, 1), key, "PK1")
+        ts(C("t3"), oc(b, t, 2), 99.0, A.mult, None, None, key, "t3")
+        ts(C("t4"), oc(b, t, 1), -16.0, A.mult, None, None, key, "t4")
+        tt(C("t3"), C("t3"), oc(b, t, 0), A.add, "t3 " + key, "t3")
+        tt(T.PK1[:, 16:32], C("t3"), C("t4"), A.add, "t3 t4", "PK1")
+
+    def norm1(To, Cc, keys):
+        pe([mm(T.TB[:, 0:256], NI, To, True, False)] + spread(T.TB, 256, Cc, False), "NIB TBC " + keys, "pTB")
+        pe(spread(T.GB, 512, T.PK1[:], True), "TBC PK1", "pGB")
+
+    def norm2(To, key):
+        ts(T.OH[:], T.GB[:, 256:512], T.PM[:], A.is_equal, None, None, "pGB PM", "OH")
+        tt(T.OHD[:], T.OH[:], T.TB[:, 0:256], A.mult, "OH pTB", "OHD")
+        pe([mm(T.TB[:, 0:256], ID, To, True, False), mm(T.TB[:, 0:256], T.ID32[:], T.OHD[:], False, True)],
+           "IDB ID32 OHD " + key, "pTB")
+
+    def norm3():
+        cp(T.XS[:], T.TB[:, 0:256], "pTB", "XS")
+        tt(T.XL[:], T.XS[:], T.GB[:, 0:256], A.mult, "XS pGB", "XL")
+
+    def merge():
+        tt(T.HX[:], T.W[:].indirect(U("EL")), T.L1[:], A.max, "W EL L1", "HX")
+        ts(T.H[:], T.HX[:], 4095, A.bitwise_and, None, None, "HX", "H")
+
+    def lengths(b, t, key):
+        tt(C("nm1"), oc(b, t, 0), oc(b, t, 2), A.subtract, key, "nm1")
+        tt(C("nm1"), C("nm1"), oc(b, t, 1), A.subtract, "nm1 " + key, "nm1")
+        ts(C("n"), C("nm1"), 1.0, A.add, None, None, "nm1", "n")
+
+    def hand_pe(t):
+        pe([mm(T.TB[:, 0:256], NI, T.XS[:], True, False)] + spread(T.TB, 256, T.c16[:], False, t == 0)
+           + ([mm(T.TB[:, 0:256], M("ROTN"), T.XL[:], False, True)] if t else []),
+           "NIB TBC XS c16" + (" XL ROTN" if t else ""), "pTB")
+        pe([mm(T.GB[:], M("LGD"), T.ZO[:], True, False)] + spread(T.GB, 512, T.PK2[:], False), "LGD ZO TBC PK2", "pGB")
+
+    def hand_v():
+        ts(T.OH[:], T.GB[:, 0:256], T.PM[:], A.is_equal, None, None, "pGB PM", "OH")
+        tt(T.OHD[:], T.OH[:], T.TB[:, 0:256], A.mult, "OH pTB", "OHD")
+        tt(T.L1[:], T.H[:], T.GB[:, 256:512], A.add, "H pGB", "L1")
+
+    def hand_u(t):
+        ms = [mm(T.TB[:, 0:256], M("REV"), T.XS[:], True, False)]
+        if t > 0:
+            ms.append(mm(T.TB[:, 0:256], M("REVD"), T.XL[:], False, False))
+        ms.append(mm(T.TB[:, 0:256], T.REV32[:], T.OHD[:], False, True))
+        pe(ms, "REV REV32 XS OHD" + (" XL REVD" if t else ""), "pTB")
+
+    def hand_dma(t):
+        act(T.UF[:], T.TB[:, 0:256], ACT.Identity, "pTB", "UF", bias=2048.0)
+        dma("y", [(T.D3[:, 0:16, :], T.UF[:]), (T.D3[:, 16:32, :], T.UF[:])], "UF", "D3", "hw%d" % t)
+        dma("y", [(T.W[:, 256 * e:256 * e + 256], T.D3[:, 15 - e:31 - e, :]) for e in range(16)], "D3", "W", "hr%d" % t)
+
+    for t in range(V):
+        ok, uk = "OC%d" % t, "OU%d" % t
+        ltk = "LT%d" % t
+        hi, lo, hit = oc("OC", t, 0), oc("OC", t, 1), oc("OC", t, 2)
+        lt = T.LT[:, 272 * t:272 * t + 272]
+        if t > 0:
+            arrive("al%d" % t, ltk)
+            arrive("ao%d" % t, ok)
+            hand_pe(t - 1)
+        gather("s", t, 0)
+        c_tail()
+        cp(T.XC[:], T.X[:].indirect(U("CL")), XALL + " CL", "XC")
+        if t == 0:
+            setup_a()
+            thresholds()
+        op("s", [lambda: g.scalar.activation(T.XC2[:, :, :, 0], T.XC[:], ACT.Identity),
+                 lambda: g.scalar.activation(T.XC2[:, :, :, 1], T.XC[:], ACT.Identity)], "XC", "XC2")
+        if t > 0:
+            hand_v()
+        gather("v", t, 1)
+        gather("s", t, 2)
+        diff(0)
+        if t > 0:
+            hand_u(t - 1)
+            hand_dma(t - 1)
+            tt(C("t1"), oc("OU", t - 1, 2), T.GOT[:], A.add, "GOT OU%d" % (t - 1), "t1")
+            tt(C("t1"), C("m1"), C("t1"), A.add, "m1 t1", "t1")
+            ts(C("m"), C("t1"), 16.0, A.min, None, None, "t1", "m")
+        c_post()
+        if t == 0:
+            gather("s", t, 3)
+            setup_b()
+        else:
+            act(T.XW[:, 4352:4608], T.X[:].indirect(T.LT[:, 272 * t + 256:272 * t + 272]), ACT.Identity, XALL + " " + ltk, "XWc")
+            gather("s", t, 3)
+        if t > 0:
+            cp(T.AINT[:], T.ACOL[:], "ACOL", "AINT")
+            ts(T.AIN2[:], T.AINT[:], 255, A.bitwise_and, None, None, "AINT", "AIN2")
+            cp(T.AF[:], T.AIN2[:], "AIN2", "AF")
+            ts(M("AI"), M("SCI"), T.AF[:], A.mult, None, None, "SCI AF", "AI")
+        ms = [mm(T.E[:], M("SCI"), T.THH[:], True, False), mm(T.E[:], M("SCI"), T.THL[:], False, False)]
+        if t > 0:
+            ms.append(mm(T.E[:], M("AI"), T.ONE[:], False, False))
+        pe(ms, "SCI THH THL" + (" AI ONE" if t else ""), "pE")
+        if t > 0:
+            ts(T.TO16[:], lt, -2048.0, A.add, None, None, ltk, "TO16")
+            lengths("OC", t, ok)
+            norm_compact("OC", t, ok)
+            norm1(T.TO16[:, 0:256], T.TO16[:, 256:272], "TO16")
+            pe([mm(T.SM[:, 0:16, :], ID, T.XW[:, 4352:4608], True, False), mm(T.SM[:, 0:16, :], NI, T.XC[:], False, True)],
+               "IDB NIB XWc XC", "pSM")
+            act(T.AB[:, :, :, 17], T.SM[:, 0:16, :], ACT.Abs, "pSM", "ABc")
+        diff(1)
+        absd(0)
+        act(T.XCB[:], T.XC[:], ACT.Identity, "XC", "XCB", bias=3071.5)
+        absd(1)
+        gather("v", t, 4)
+        if t == 0:
+            lengths("OC", t, ok)
+        else:
+            norm2(T.TO16[:, 0:256], "TO16")
+        pe([mm(T.SM[:, 0:16, s], ID, hi, True, True) for s in range(16)], "IDB " + ok, "pSM")
+        dsum(0)
+        if t > 0:
+            norm3()
+        j = 2 if (t + 1) % len(T.cores) == 0 else 1
+        GR, GRR = "GR%d" % j, "GRR%d" % j
+        if t < V - 1:
+            ms = [mm(T.TB[:, 0:256], M(GR), T.XS[:], True, t == 0)]
+            if t > 0:
+                ms.append(mm(T.TB[:, 0:256], M(GRR), T.XL[:], False, True))
+            ms.append(mm(T.TB[:, 256:272], M(GR), T.c16[:], True, True))
+            pe(ms, "%s XS c16" % GR + (" XL " + GRR if t else ""), "pTB")
+        else:
+            pe([mm(T.TB[:, 0:256], ID, T.XS[:], True, False), mm(T.TB[:, 0:256], M("ROTD"), T.XL[:], False, True)],
+               "IDB ROTD XS XL", "pTB")
+        diff(2)
+        tt(T.DEAD[:, :, 1:17], T.SM[:, 0:16, :], T.SCN[:], A.is_le, "pSM SCN", "DEAD")
+        if t == 0:
+            setup_c()
+        dsum(1)
+        pe([mm(T.E[:], M("PENI"), T.DEAD[:], False, False), mm(T.E[:, 1:288:18], M("PENI"), lo, False, False),
+            mm(T.E[:, 17:288:18], M("PENI"), hit, False, False)], "PENI DEAD " + ok, "pE")
+        absd(2)
+        if t < V - 1:
+            ts(T.SD[:, 272 * t:272 * t + 272], T.TB[:, 0:272], 2048.0, A.add, None, None, "pTB", "SD%d" % t)
+            remote(T.LT[:, 272 * t + 272:272 * t + 544], T.SD[:, 272 * t:272 * t + 272], "al%d" % (t + 1), "SD%d" % t)
+        else:
+            cp(T.T5B[:], T.TB[:, 0:256], "pTB", "T5B")
+        diff(3)
+        tt(C("kc"), C("KCB"), lo, A.add, "KCB " + ok, "kc")
+        tt(C("b0"), C("DD"), hit, A.mult, "DD " + ok, "b0")
+        tt(C("b0"), C("b0"), C("DN"), A.add, "b0 DN", "b0")
+        ts(C("t2"), hi, 0.0, A.is_le, None, None, ok, "t2")
+        tt(C("b0"), C("b0"), C("t2"), A.mult, "b0 t2", "b0")
+        tt(C("b0"), C("b0"), C("kc"), A.add, "b0 kc", "b0")
+        ts(U("BL"), C("b0"), -256.0, A.add, None, None, "b0", "BL")
+        tt(T.D0B[:], T.XW[:, 256:4624].indirect(U("BL")), T.XC[:], A.subtract, XWK + " XWc XWz BL XC", "D0B")
+        absd(3)
+        dsum(2)
+        act(T.A0B[:], T.D0B[:], ACT.Abs, "D0B", "A0B", scale=2.0)
+        pe([mm(T.D0[:, 0, :, :], ID, T.A0B[:], True, False), mm(T.D0[:, 0, :, :], NI, T.XC[:], False, True)], "IDB NIB A0B XC", "pD0")
+        act(T.XW[:, 0:256], T.D0[:, 0, :, :], ACT.Identity, "pD0", "XWB", bias=0.5)
+        ts(C("n16"), C("nm1"), 15.0, A.is_equal, None, None, "nm1", "n16")
+        ts(C("t3"), C("n16"), -16.0, A.mult, 1.0, A.add, "n16", "t3")
+        tt(T.PK2[:, 0:16], C("t3"), C("nm1"), A.add, "t3 nm1", "PK2")
+        ts(T.PK2[:, 16:32], C("m1"), 8192.0, A.mult, None, None, "m1", "PK2")
+        ts(M("LGD"), ID, T.LGS[:, t:t + 1], A.mult, None, None, "IDB LGS", "LGD")
+        if t > 0:
+            merge()
+        if t < V - 1:
+            ts(T.HM[:], T.H[:], -2048.0, A.add, RM(t + 1), A.mult, "H RM", "HM")
+            pe([mm(T.SM[:, 16, :], T.TIND[:, r, :], T.HM[:, r:256:16], r == 0, r == 15) for r in range(16)], "TIND HM", "pSM")
+        tt(C("t4"), C("m1"), C("nm1"), A.add, "m1 nm1", "t4")
+        ts(C("t4"), C("t4"), float(t + 2), A.add, 256.0, A.mult, "t4", "t4")
+        tt(I("e1"), C("t4"), C("IC"), A.add, "t4 IC", "e1")
+        ts(I("e2"), I("e1"), 4095, A.bitwise_and, None, None, "e1", "e2")
+        cp(U("EL"), I("e2"), "e2", "EL")
+        if t == V - 1:
+            hand_pe(t)
+            hand_v()
+        dsum(3, True)
+        if t < V - 1:
+            tt(C("q"), T.SM[:, 16, :], T.c16[:], A.subtract, "pSM c16", "q")
+            ts(C("t3"), C("m1"), 0.0, A.is_gt, None, None, "m1", "t3")
+            tt(C("q"), C("q"), C("t3"), A.mult, "q t3", "q")
+            tt(C("q"), C("q"), C("cf"), A.add, "q cf", "q")
+        else:
+            hand_u(t)
+            hand_dma(t)
+        op("v", lambda: g.vector.tensor_tensor_scan(T.R[:], T.E[:], T.VC[:], 0.0, A.max, A.min), "pE VC", "R")
+        cp(U("ZL"), T.R[:, 17:288:18], "R", "ZL")
+        tt(T.Y2[:], T.XW[:].indirect(U("ZL")), T.XCB[:], A.add, XWK + " XWc XWz XWB ZL XCB", "Y2")
+        pe([mm(T.GB[:, 0:16], T.TW[:, r, :], T.Y2[:, r:256:16], r == 0, r == 15) for r in range(16)], "TW Y2", "pGB")
+        tt(C("kz"), T.R[:, 17:288:18], C("kc"), A.subtract, "R kc", "kz")
+        tt(C("k"), C("kz"), C("nm1"), A.min, "kz nm1", "k")
+        ts(oc("OU", t, 2), C("kz"), 0.0, A.is_ge, None, None, "kz", uk)
+        tt(C("g0"), C("n"), C("k"), A.subtract, "n k", "g0")
+        tt(T.GOT[:], C("g0"), oc("OU", t, 2), A.mult, "g0 " + uk, "GOT")
+        tt(oc("OU", t, 1), C("n16"), oc("OU", t, 2), A.is_gt, "n16 " + uk, uk)
+        tt(oc("OU", t, 0), C("n"), T.GOT[:], A.subtract, "n GOT", uk)
+        if t < V - 1:
+            pe([mm(T.SM[:, 17, :], M("ONB"), T.GOT[:], True, True),
+                mm(T.SM[:, 20:23, :], M(GR), T.OU[:, 3 * t:3 * t + 3, :], True, True)], "ONB GOT %s %s" % (GR, uk), "pSM")
+        ts(T.YB[:], T.Y2[:], 0.5, A.mult, -1536.0, A.add, "Y2", "YB")
+        cp(I("z1"), T.GB[:, 0:16], "pGB", "z1")
+        ts(I("z2"), I("z1"), 15, A.bitwise_and, None, None, "z1", "z2")
+        tt(C("z3"), I("z2"), C("IC16"), A.add, "z2 IC16", "z3")
+        cp(U("SL"), C("z3"), "z3", "SL")
+        cp(T.X[:].indirect(U("SL")), T.YB[:], "YB SL X Xh", "X")
+        if t < V - 1:
+            op("v", lambda: g.vector.tensor_reduce(T.ACOL[:], T.SM[:, 17, :], AxisListType.X, A.add), "pSM", "ACOL")
+            cp(T.OS[:, 3 * t:3 * t + 3, :], T.SM[:, 20:23, :], "pSM", "OS%d" % t)
+            remote(T.OC[:, 3 * t + 3:3 * t + 6, :], T.OS[:, 3 * t:3 * t + 3, :], "ao%d" % (t + 1), "OS%d" % t)
+            ts(I("fi"), C("IC37"), T.ACOL[:], A.add, float(613 * (t + 1)), A.add, "IC37 ACOL", "fi")
+            ts(I("fj"), I("fi"), 4095, A.bitwise_and, None, None, "fi", "fj")
+            tt(C("na"), C("p0"), oc("OU", t, 2), A.is_gt, "p0 " + uk, "na")
+        if t == 0:
+            setup_d()
+
+    t, uk = V - 1, "OU%d" % (V - 1)
+    dma("y", [(T.yx[:, 0:2048], T.X[:, 0:2048])], XALL, "yx", "ox")
+    dma("s", [(T.yx[:, 2048:4096], T.X[:, 2048:4096])], XALL, "yx2", "ox2")
+    tt(C("t1"), oc("OU", t, 2), T.GOT[:], A.add, "GOT " + uk, "t1")
+    tt(C("t1"), C("m1"), C("t1"), A.add, "m1 t1", "t1")
+    ts(T.PK2[:, 0:16], C("t1"), 16.0, A.min, None, None, "t1", "PK2")
+    norm_compact("OU", t, uk)
+    norm1(T.T5B[:], T.c16[:], "T5B c16")
+    lengths("OU", t, uk)
+    cp(T.PK2[:, 16:32], C("n"), "n", "PK2")
+    norm2(T.T5B[:], "T5B")
+    norm3()
+    pe(spread(T.GB, 512, T.PK2[:], True), "TBC PK2", "pGB")
+    pe([mm(T.TB[:, 0:256], ID, T.XS[:], True, False), mm(T.TB[:, 0:256], M("ROTD"), T.XL[:], False, True)], "IDB ROTD XS XL", "pTB")
+    act(T.YM[:], T.GB[:], ACT.Identity, "pGB", "YM")
+    dma("y", [(T.ym[:], T.YM[0:128:16, 0:256]), (T.yn[:], T.YM[0:128:16, 256:512])], "YM", "ym yn", "om")
+    act(T.YTF[:], T.TB[:, 0:256], ACT.Identity, "pTB", "YTF", bias=2048.0)
+    ts(T.TSB[:], T.YM[:, 256:512], T.PM[:], A.is_gt, None, None, "YM PM", "TSB")
+    tt(T.YT[:], T.YTF[:], T.TSB[:], A.mult, "YTF TSB", "YT")
+    dma("s", [(T.yt[:], T.YT[:])], "YT", "yt", "oy")
+    ts(T.TSB[:], T.YM[:, 0:256], T.LGF[:, V - 1:V], A.is_gt, None, None, "YM LGF", "TSB")
+    merge()
+    tt(T.HF[:], T.H[:], T.TSB[:], A.mult, "H TSB", "HF")
+    pe([mm(T.TB[:, 0:256], T.ROT6[:], T.HF[:], True, True)], "ROT6 HF", "pTB")
+    cp(T.YH[:], T.TB[:, 0:256], "pTB", "YH")
+    dma("y", [(T.yh[:], T.YH[:])], "YH", "yh", "oh")
+    for s in sorted(cnt):
+        if clk["g"].get(s, 0) < cnt[s]:
+            g.wait_ge(T.sem[s], cnt[s])

@@ -1,5 +1,5 @@
 import numpy as np
-from concourse.mybir import AluOpType, AxisListType, ActivationFunctionType
+from concourse.mybir import AluOpType, ActivationFunctionType
 
 V = 6
 SCRATCH = {}
@@ -10,10 +10,10 @@ def _sb(names, shape, dtype, where="sbuf"):
         SCRATCH[nm] = (where, shape, dtype)
 
 
-_CF = ("m m1 q cf na d nm1 n kc t1 t2 t3 t4 kz k g0 n16 b0 z3 p0 IC IC37 IC16 KCB DN DD ROW RM").split()
+_CF = ("m m1 q cf na d nm1 n kc t1 t2 t3 t4 kz k g0 n16 b0 z3 p0 u1 u2 t7 t8 t9 IC IC37 IC16 KCB DN DD ROW RM").split()
 _CI = "fi fj z1 z2 e1 e2".split()
 _CU = "CL ZL SL EL BL".split()
-_MB = "IDB NIB SCI PENI GM REV ROTD REVD AI LGD ONB GR1 GR2 GRR1 GRR2 ZZB R6A R6B ROTN".split()
+_MB = "IDB NIB SCI PENI GM REV ROTD REVD AI LGD ONB GR1 GR2 GRR1 GRR2 ZZB R6A R6B ROTN NI2".split()
 _sb("X", [128, 4096], "bfloat16")
 _sb("XW", [128, 4624], "bfloat16")
 _sb("AB", [128, 16, 16, 18], "bfloat16")
@@ -23,7 +23,7 @@ _sb("XCB OHD L1 UF HF YTF TSB YH YT", [128, 256], "float32")
 _sb("Y2 XS XL HM T5B", [128, 256], "float16")
 _sb("TO16", [128, 272], "float16")
 _sb("DEAD", [128, 16, 18], "bfloat16")
-_sb("SCN", [128, 16, 16], "float32")
+_sb("SCN", [128, 16, 16], "bfloat16")
 _sb("H HX TR MTI", [128, 256], "int32")
 _sb("W", [128, 4096], "float32")
 _sb("D3", [8, 32, 256], "float32", "dram")
@@ -58,6 +58,14 @@ _sb("SM", [128, 32, 16], "float32", "psum")
 SEMAPHORES = (["sv", "ss", "sp", "sg", "ls", "lx0", "lx1", "lh", "lt", "lm", "lw", "ox", "ox2", "oh", "oy", "om"]
               + ["hw%d" % t for t in range(V)] + ["hr%d" % t for t in range(V)]
               + ["al%d" % t for t in range(1, V)] + ["ao%d" % t for t in range(1, V)])
+BIGV = {"XW0": 1.4, "XW1": 1.4, "XW2": 1.4, "XW3": 1.4, "XC": 0.43, "Y2": 0.45, "D0B": 0.45, "HX": 0.45, "X": 0.75, "R": 0.3,
+        "OH": 0.27, "OHD": 0.27, "L1": 0.27, "XS": 0.47, "XL": 0.27, "LT0": 0.27, "TO16": 0.18, "DEAD": 0.27, "H": 0.27, "HM": 0.27,
+        "XC2": 0.3, "TIND": 0.9, "TINM": 0.9, "TW": 0.9, "MT": 0.7, "MTB": 0.3, "MTI": 0.27, "ZO": 0.2}
+BIGS = {"XW0": 1.4, "XW1": 1.4, "XW2": 1.4, "XW3": 1.4, "AB0": 0.95, "AB1": 0.95, "AB2": 0.95, "AB3": 0.95, "XC2": 0.6, "ABc": 0.3,
+        "XCB": 0.3, "UF": 0.3, "A0B": 0.3, "XWB": 0.3, "YB": 0.3, "DEAD": 0.3, "LGD": 0.2, "AI": 0.2, "XWc": 0.42, "THH": 0.32, "THL": 0.32, "YM": 0.5, "YTF": 0.3}
+TRIES = 400
+CHOSEN = {}
+LOG = []
 PS = {"pD0", "pD1", "pE", "pGB", "pTB", "pSM"}
 
 
@@ -109,22 +117,106 @@ def rank_program(g, core, T, topo):
             lastw[k] = (s, v)
             acc[k] = {s: v} if k in PS else {}
 
+    prog = []
+
     def op(q, fns, R, W):
-        R, W = R.split(), W.split()
-        need(q, R, W)
-        s = own[q]
-        for f in (fns if isinstance(fns, list) else [fns]):
-            f().then_inc(T.sem[s], 1)
-            cnt[s] = cnt.get(s, 0) + 1
-        done(q, s, cnt[s], R, W)
+        prog.append((q, "c", fns if isinstance(fns, list) else [fns], R.split(), W.split(), own[q]))
 
     def dma(q, pairs, R, W, s):
-        R, W = R.split(), W.split()
-        need(q, R, W)
-        for o, i in pairs:
-            eng[q].dma_start(o, i).then_inc(T.sem[s], 16)
-            cnt[s] = cnt.get(s, 0) + 16
+        prog.append((q, "d", pairs, R.split(), W.split(), s))
+
+    def emit(q, kind, fns, R, W, s):
+        need(q, R, W if kind != "r" else [])
+        if kind == "r":
+            fns[0]()
+            return
+        for f in fns:
+            if kind == "c":
+                f().then_inc(T.sem[s], 1)
+            else:
+                eng[q].dma_start(f[0], f[1]).then_inc(T.sem[s], 16)
+            cnt[s] = cnt.get(s, 0) + (1 if kind == "c" else 16)
         done(q, s, cnt[s], R, W)
+
+    def guess(q, kind, fns, W):
+        w = W[0]
+        if kind == "r":
+            return 1.0, 3.5
+        if kind == "d":
+            return 0.1 * len(fns), 6.0 if w in ("X", "Xh") else 2.5
+        if q == "p":
+            return 0.03 * len(fns), 0.08
+        if q == "g":
+            return 0.8, 0.1
+        big = BIGS if q == "s" else BIGV
+        return 0.1 + (big.get(w, 0.15 if q == "s" else 0.1) if len(fns) < 3 else 0.09 * len(fns)), 0.06
+
+    def order():
+        n = len(prog)
+        if n in CHOSEN:
+            return CHOSEN[n]
+        succ, npred = [[] for _ in range(n)], [0] * n
+        lw, rd, ps = {}, {}, {}
+        dur = [guess(p[0], p[1], p[2], p[4]) for p in prog]
+        for i, (q, kind, fns, R, W, s) in enumerate(prog):
+            pre = set()
+            for k in R:
+                if k in lw:
+                    pre.add(lw[k])
+            for k in W:
+                if k in lw:
+                    pre.add(lw[k])
+                pre.update(rd.get(k, ()))
+            for k in R + W:
+                if k in PS:
+                    pre.update(j for qq, j in ps.get(k, {}).items() if qq != q)
+                    ps.setdefault(k, {})[q] = i
+            for k in R:
+                rd.setdefault(k, []).append(i)
+            for k in W:
+                lw[k], rd[k] = i, []
+            pre.discard(i)
+            for j in pre:
+                succ[j].append(i)
+            npred[i] = len(pre)
+        tail = [0.0] * n
+        for i in range(n - 1, -1, -1):
+            tail[i] = dur[i][0] + max([dur[i][1] + tail[j] for j in succ[i]] or [0.0])
+
+        def play(key):
+            left = list(npred)
+            ready = {q: [] for q in eng}
+            at = [0.0] * n
+            for i in range(n):
+                if left[i] == 0:
+                    ready[prog[i][0]].append(i)
+            free = {q: 0.0 for q in eng}
+            out, end = [], 0.0
+            while len(out) < n:
+                st, q = min((max(free[q], min(at[i] for i in ready[q])), q) for q in eng if ready[q])
+                i = max([j for j in ready[q] if at[j] <= st + 0.02], key=lambda j: key[j])
+                ready[q].remove(i)
+                st = max(st, at[i])
+                free[q] = st + dur[i][0]
+                end = max(end, free[q] + dur[i][1])
+                out.append(i)
+                for j in succ[i]:
+                    at[j] = max(at[j], free[q] + dur[i][1])
+                    left[j] -= 1
+                    if left[j] == 0:
+                        ready[prog[j][0]].append(j)
+            return end, out
+        best = None
+        for k in range(TRIES):
+            rng = np.random.default_rng(k)
+            a = float(rng.uniform(0.02, 0.3)) if k else 1.0
+            noise = rng.normal(0.0, float(rng.uniform(0.0, 3.0)) if k else 0.0, n)
+            got = play([float(tail[i] - a * i + noise[i]) for i in range(n)])
+            if best is None or got[0] < best[0]:
+                best = got + (k, a)
+        LOG.append(best[2:] + best[:1])
+        CHOSEN[n] = best[1]
+        return best[1]
 
     def arrive(s, k):
         cnt[s] = neng
@@ -155,10 +247,10 @@ def rank_program(g, core, T, topo):
     def fill(ap, c, W):
         op("v", lambda: g.vector.memset(ap, c), "", W)
 
-    def remote(dst, src, rs, key):
-        need("g", [key], [])
+    def remote(dst, src, rs, key, lands):
         rid, pid, _ = topo.addr(nxt)
-        g.remote_dma(dst, src, T.sem[rs], T.sem["ls"], pid, rid, topo.mask(core, nxt))
+        prog.append(("g", "r", [lambda: g.remote_dma(dst, src, T.sem[rs], T.sem["ls"], pid, rid, topo.mask(core, nxt))],
+                     [key], [lands], "ls"))
         cnt["ls"] = cnt.get("ls", 0) + neng
 
     def C(n):
@@ -203,7 +295,7 @@ def rank_program(g, core, T, topo):
     pick(M("GM"), M("ZZB"), [[16, 8], [0, 16]], A.is_ge, 15, -1, "ZZB", "GM")
     pick(ID, M("ONB"), [[-1, 128]], A.is_equal, 0, 1, "ONB", "IDB")
     iota(T.VC[:], [[256, 16], [1, 18]], 255, 0, "VC", True)
-    iota(T.SCN[:], [[0, 16], [1, 16]], 0, 0, "SCN", True)
+    iota(T.SCN[:], [[0, 16], [1, 16]], 1, 0, "SCN", True)
     iota(T.LGI[:], [[-1, 8]], 15, 1, "LGI", False)
     pick(M("REV"), M("ONB"), [[-16, 8], [1, 16]], A.is_equal, -15, 1, "ONB", "REV")
     pick(T.REV32[:], T.ONF[:], [[-16, 8], [1, 16]], A.is_equal, -15, 1, "ONF", "REV32")
@@ -245,8 +337,8 @@ def rank_program(g, core, T, topo):
 
     def c_post():
         ts(T.c16[:], C("cf"), -2048.0, A.add, None, None, "cf", "c16")
-        ts(C("m1"), C("m"), -1.0, A.add, 0.0, A.max, "m", "m1")
-        ts(C("p0"), C("m1"), 0.0, A.is_le, None, None, "m1", "p0")
+        act(C("m1"), C("m"), ACT.Relu, "m", "m1", bias=-1.0)
+        act(C("p0"), C("m1"), ACT.Relu, "m1", "p0", scale=-1.0, bias=1.0)
 
     def setup_a():
         cp(T.OC[:, 0, :], T.CP[:, 1, :], "CP", "OC0")
@@ -261,6 +353,7 @@ def rank_program(g, core, T, topo):
         ts(T.TINM[:], T.TIND[:], -8192.0, A.mult, None, None, "TIND", "TINM")
         ts(T.XS[:], T.TR[:], -2048.0, A.add, None, None, "TR", "XS")
         fill(T.XW[:, 4352:4624], 0.0, "XWc XWz")
+        ts(C("DD"), C("IC"), -1.0, A.mult, 256.0, A.add, "IC", "DD")
         fill(T.AB[:, :, :, 0], 0.0, "ABz")
         fill(T.AB[:, :, :, 17], 0.0, "ABc")
         for nm, j, src in (("GR1", 1, "IDB"), ("GR2", 2, "IDB")):
@@ -268,7 +361,6 @@ def rank_program(g, core, T, topo):
             cp(M(nm, 0, 16 * j), M(src, 128 - 16 * j, 128), src, nm)
         ts(C("IC16"), C("IC"), 16.0, A.mult, None, None, "IC", "IC16")
         ts(C("KCB"), C("IC16"), 256.0, A.add, None, None, "IC16", "KCB")
-        ts(C("DD"), C("IC"), -1.0, A.mult, 256.0, A.add, "IC", "DD")
         ts(C("DN"), C("IC"), -15.0, A.mult, 4096.0, A.add, "IC", "DN")
         ts(T.PM16[:], T.PM[:], 16.0, A.mult, None, None, "PM", "PM16")
         ts(T.VC[:], T.VC[:], T.PM16[:], A.add, None, None, "VC PM16", "VC")
@@ -308,13 +400,11 @@ def rank_program(g, core, T, topo):
         act(T.THL[:], T.E[:], ACT.Identity, "pE", "THL")
         fill(T.THH[:, 0:288:18], 4080.0, "THH")
 
-    XWK = "XW0 XW1 XW2 XW3 XW4"
-    PIECE = {0: (0, 64), 1: (64, 128), 2: (128, 192), 3: (192, 224), 4: (224, 256)}
+    XWK = "XW0 XW1 XW2 XW3 XWc"
 
     def gather(q, t, b):
-        lo, hi = PIECE[b]
-        w = T.X[:].indirect(T.LT[:, 272 * t + lo:272 * t + hi])
-        o = T.XW[:, 256 + 16 * lo:256 + 16 * hi]
+        w = T.X[:].indirect(T.LT[:, 272 * t + 64 * b:272 * t + 64 * b + 64])
+        o = T.XW[:, 256 + 1024 * b:1280 + 1024 * b]
         if q == "s":
             act(o, w, ACT.Identity, XALL + " LT%d" % t, "XW%d" % b)
         else:
@@ -328,7 +418,7 @@ def rank_program(g, core, T, topo):
             for s in range(8):
                 ms.append(mm(D[:, 2 * h:2 * h + 2, :, 2 * s:2 * s + 2], NI,
                              T.XC2[:, 4 * b + 2 * h:4 * b + 2 * h + 2, :, :], False, s == 7))
-        pe(ms, "IDB NIB XC2 XW%d" % b + (" XW4" if b == 3 else ""), "pD%d" % (b % 2))
+        pe(ms, "IDB NIB XC2 XW%d" % b, "pD%d" % (b % 2))
 
     def absd(b):
         act(T.AB[:, 4 * b:4 * b + 4, :, 1:17], T["D%d" % (b % 2)][:], ACT.Abs, "pD%d" % (b % 2), "AB%d" % b)
@@ -344,11 +434,11 @@ def rank_program(g, core, T, topo):
         return T[b][:, 3 * t + k, :]
 
     def norm_compact(b, t, key):
-        cp(T.PK1[:, 0:16], oc(b, t, 1), key, "PK1")
-        ts(C("t3"), oc(b, t, 2), 99.0, A.mult, None, None, key, "t3")
-        ts(C("t4"), oc(b, t, 1), -16.0, A.mult, None, None, key, "t4")
+        act(T.PK1[:, 0:16], oc(b, t, 1), ACT.Identity, key, "PK1")
+        act(C("t3"), oc(b, t, 2), ACT.Identity, key, "t3", scale=99.0)
+        act(C("t7"), oc(b, t, 1), ACT.Identity, key, "t7", scale=-16.0)
         tt(C("t3"), C("t3"), oc(b, t, 0), A.add, "t3 " + key, "t3")
-        tt(T.PK1[:, 16:32], C("t3"), C("t4"), A.add, "t3 t4", "PK1")
+        tt(T.PK1[:, 16:32], C("t3"), C("t7"), A.add, "t3 t7", "PK1")
 
     def norm1(To, Cc, keys):
         pe([mm(T.TB[:, 0:256], NI, To, True, False)] + spread(T.TB, 256, Cc, False), "NIB TBC " + keys, "pTB")
@@ -357,11 +447,7 @@ def rank_program(g, core, T, topo):
     def norm2(To, key):
         ts(T.OH[:], T.GB[:, 256:512], T.PM[:], A.is_equal, None, None, "pGB PM", "OH")
         tt(T.OHD[:], T.OH[:], T.TB[:, 0:256], A.mult, "OH pTB", "OHD")
-        pe([mm(T.TB[:, 0:256], ID, To, True, False), mm(T.TB[:, 0:256], T.ID32[:], T.OHD[:], False, True)],
-           "IDB ID32 OHD " + key, "pTB")
-
-    def norm3():
-        cp(T.XS[:], T.TB[:, 0:256], "pTB", "XS")
+        tt(T.XS[:], To, T.OHD[:], A.add, "OHD " + key, "XS")
         tt(T.XL[:], T.XS[:], T.GB[:, 0:256], A.mult, "XS pGB", "XL")
 
     def merge():
@@ -371,7 +457,7 @@ def rank_program(g, core, T, topo):
     def lengths(b, t, key):
         tt(C("nm1"), oc(b, t, 0), oc(b, t, 2), A.subtract, key, "nm1")
         tt(C("nm1"), C("nm1"), oc(b, t, 1), A.subtract, "nm1 " + key, "nm1")
-        ts(C("n"), C("nm1"), 1.0, A.add, None, None, "nm1", "n")
+        act(C("n"), C("nm1"), ACT.Identity, "nm1", "n", bias=1.0)
 
     def hand_pe(t):
         pe([mm(T.TB[:, 0:256], NI, T.XS[:], True, False)] + spread(T.TB, 256, T.c16[:], False, t == 0)
@@ -402,8 +488,6 @@ def rank_program(g, core, T, topo):
         hi, lo, hit = oc("OC", t, 0), oc("OC", t, 1), oc("OC", t, 2)
         lt = T.LT[:, 272 * t:272 * t + 272]
         if t > 0:
-            arrive("al%d" % t, ltk)
-            arrive("ao%d" % t, ok)
             hand_pe(t - 1)
         gather("s", t, 0)
         c_tail()
@@ -411,8 +495,7 @@ def rank_program(g, core, T, topo):
         if t == 0:
             setup_a()
             thresholds()
-        op("s", [lambda: g.scalar.activation(T.XC2[:, :, :, 0], T.XC[:], ACT.Identity),
-                 lambda: g.scalar.activation(T.XC2[:, :, :, 1], T.XC[:], ACT.Identity)], "XC", "XC2")
+        op("v", [(lambda e=e: g.vector.tensor_copy(T.XC2[:, :, :, e], T.XC[:])) for e in range(2)], "XC", "XC2")
         if t > 0:
             hand_v()
         gather("v", t, 1)
@@ -420,22 +503,21 @@ def rank_program(g, core, T, topo):
         diff(0)
         if t > 0:
             hand_u(t - 1)
-            hand_dma(t - 1)
             tt(C("t1"), oc("OU", t - 1, 2), T.GOT[:], A.add, "GOT OU%d" % (t - 1), "t1")
             tt(C("t1"), C("m1"), C("t1"), A.add, "m1 t1", "t1")
             ts(C("m"), C("t1"), 16.0, A.min, None, None, "t1", "m")
         c_post()
         if t == 0:
-            gather("s", t, 3)
             setup_b()
         else:
+            hand_dma(t - 1)
             act(T.XW[:, 4352:4608], T.X[:].indirect(T.LT[:, 272 * t + 256:272 * t + 272]), ACT.Identity, XALL + " " + ltk, "XWc")
-            gather("s", t, 3)
+        gather("s", t, 3)
         if t > 0:
             cp(T.AINT[:], T.ACOL[:], "ACOL", "AINT")
             ts(T.AIN2[:], T.AINT[:], 255, A.bitwise_and, None, None, "AINT", "AIN2")
             cp(T.AF[:], T.AIN2[:], "AIN2", "AF")
-            ts(M("AI"), M("SCI"), T.AF[:], A.mult, None, None, "SCI AF", "AI")
+            act(M("AI"), M("SCI"), ACT.Identity, "SCI AF", "AI", scale=T.AF[:])
         ms = [mm(T.E[:], M("SCI"), T.THH[:], True, False), mm(T.E[:], M("SCI"), T.THL[:], False, False)]
         if t > 0:
             ms.append(mm(T.E[:], M("AI"), T.ONE[:], False, False))
@@ -448,19 +530,18 @@ def rank_program(g, core, T, topo):
             pe([mm(T.SM[:, 0:16, :], ID, T.XW[:, 4352:4608], True, False), mm(T.SM[:, 0:16, :], NI, T.XC[:], False, True)],
                "IDB NIB XWc XC", "pSM")
             act(T.AB[:, :, :, 17], T.SM[:, 0:16, :], ACT.Abs, "pSM", "ABc")
-        diff(1)
         absd(0)
+        diff(1)
         act(T.XCB[:], T.XC[:], ACT.Identity, "XC", "XCB", bias=3071.5)
         absd(1)
-        gather("v", t, 4)
+        pe([mm(T.SM[:, 0:16, :], ID, T.SCN[:], True, False)] + [mm(T.SM[:, 0:16, s], NI, hi, False, s == 15) for s in range(16)],
+           "IDB NIB SCN " + ok, "pSM")
+        diff(2)
         if t == 0:
             lengths("OC", t, ok)
         else:
             norm2(T.TO16[:, 0:256], "TO16")
-        pe([mm(T.SM[:, 0:16, s], ID, hi, True, True) for s in range(16)], "IDB " + ok, "pSM")
         dsum(0)
-        if t > 0:
-            norm3()
         j = 2 if (t + 1) % len(T.cores) == 0 else 1
         GR, GRR = "GR%d" % j, "GRR%d" % j
         if t < V - 1:
@@ -472,8 +553,7 @@ def rank_program(g, core, T, topo):
         else:
             pe([mm(T.TB[:, 0:256], ID, T.XS[:], True, False), mm(T.TB[:, 0:256], M("ROTD"), T.XL[:], False, True)],
                "IDB ROTD XS XL", "pTB")
-        diff(2)
-        tt(T.DEAD[:, :, 1:17], T.SM[:, 0:16, :], T.SCN[:], A.is_le, "pSM SCN", "DEAD")
+        act(T.DEAD[:, :, 1:17], T.SM[:, 0:16, :], ACT.Relu, "pSM", "DEAD")
         if t == 0:
             setup_c()
         dsum(1)
@@ -482,7 +562,7 @@ def rank_program(g, core, T, topo):
         absd(2)
         if t < V - 1:
             ts(T.SD[:, 272 * t:272 * t + 272], T.TB[:, 0:272], 2048.0, A.add, None, None, "pTB", "SD%d" % t)
-            remote(T.LT[:, 272 * t + 272:272 * t + 544], T.SD[:, 272 * t:272 * t + 272], "al%d" % (t + 1), "SD%d" % t)
+            remote(T.LT[:, 272 * t + 272:272 * t + 544], T.SD[:, 272 * t:272 * t + 272], "al%d" % (t + 1), "SD%d" % t, "LT%d" % (t + 1))
         else:
             cp(T.T5B[:], T.TB[:, 0:256], "pTB", "T5B")
         diff(3)
@@ -493,24 +573,24 @@ def rank_program(g, core, T, topo):
         tt(C("b0"), C("b0"), C("t2"), A.mult, "b0 t2", "b0")
         tt(C("b0"), C("b0"), C("kc"), A.add, "b0 kc", "b0")
         ts(U("BL"), C("b0"), -256.0, A.add, None, None, "b0", "BL")
-        tt(T.D0B[:], T.XW[:, 256:4624].indirect(U("BL")), T.XC[:], A.subtract, XWK + " XWc XWz BL XC", "D0B")
+        tt(T.D0B[:], T.XW[:, 256:4624].indirect(U("BL")), T.XC[:], A.subtract, XWK + " XWz BL XC", "D0B")
         absd(3)
         dsum(2)
         act(T.A0B[:], T.D0B[:], ACT.Abs, "D0B", "A0B", scale=2.0)
         pe([mm(T.D0[:, 0, :, :], ID, T.A0B[:], True, False), mm(T.D0[:, 0, :, :], NI, T.XC[:], False, True)], "IDB NIB A0B XC", "pD0")
         act(T.XW[:, 0:256], T.D0[:, 0, :, :], ACT.Identity, "pD0", "XWB", bias=0.5)
-        ts(C("n16"), C("nm1"), 15.0, A.is_equal, None, None, "nm1", "n16")
-        ts(C("t3"), C("n16"), -16.0, A.mult, 1.0, A.add, "n16", "t3")
-        tt(T.PK2[:, 0:16], C("t3"), C("nm1"), A.add, "t3 nm1", "PK2")
-        ts(T.PK2[:, 16:32], C("m1"), 8192.0, A.mult, None, None, "m1", "PK2")
-        ts(M("LGD"), ID, T.LGS[:, t:t + 1], A.mult, None, None, "IDB LGS", "LGD")
+        act(C("n16"), C("nm1"), ACT.Relu, "nm1", "n16", bias=-14.0)
+        act(C("t8"), C("n16"), ACT.Identity, "n16", "t8", scale=-16.0, bias=1.0)
+        tt(T.PK2[:, 0:16], C("t8"), C("nm1"), A.add, "t8 nm1", "PK2")
+        act(T.PK2[:, 16:32], C("m1"), ACT.Identity, "m1", "PK2", scale=8192.0)
+        act(M("LGD"), ID, ACT.Identity, "IDB LGS", "LGD", scale=T.LGS[:, t:t + 1])
         if t > 0:
             merge()
         if t < V - 1:
             ts(T.HM[:], T.H[:], -2048.0, A.add, RM(t + 1), A.mult, "H RM", "HM")
             pe([mm(T.SM[:, 16, :], T.TIND[:, r, :], T.HM[:, r:256:16], r == 0, r == 15) for r in range(16)], "TIND HM", "pSM")
         tt(C("t4"), C("m1"), C("nm1"), A.add, "m1 nm1", "t4")
-        ts(C("t4"), C("t4"), float(t + 2), A.add, 256.0, A.mult, "t4", "t4")
+        act(C("t4"), C("t4"), ACT.Identity, "t4", "t4", scale=256.0, bias=256.0 * (t + 2))
         tt(I("e1"), C("t4"), C("IC"), A.add, "t4 IC", "e1")
         ts(I("e2"), I("e1"), 4095, A.bitwise_and, None, None, "e1", "e2")
         cp(U("EL"), I("e2"), "e2", "EL")
@@ -520,15 +600,15 @@ def rank_program(g, core, T, topo):
         dsum(3, True)
         if t < V - 1:
             tt(C("q"), T.SM[:, 16, :], T.c16[:], A.subtract, "pSM c16", "q")
-            ts(C("t3"), C("m1"), 0.0, A.is_gt, None, None, "m1", "t3")
-            tt(C("q"), C("q"), C("t3"), A.mult, "q t3", "q")
+            act(C("u1"), C("p0"), ACT.Identity, "p0", "u1", scale=-1.0, bias=1.0)
+            tt(C("q"), C("q"), C("u1"), A.mult, "q u1", "q")
             tt(C("q"), C("q"), C("cf"), A.add, "q cf", "q")
         else:
             hand_u(t)
             hand_dma(t)
         op("v", lambda: g.vector.tensor_tensor_scan(T.R[:], T.E[:], T.VC[:], 0.0, A.max, A.min), "pE VC", "R")
         cp(U("ZL"), T.R[:, 17:288:18], "R", "ZL")
-        tt(T.Y2[:], T.XW[:].indirect(U("ZL")), T.XCB[:], A.add, XWK + " XWc XWz XWB ZL XCB", "Y2")
+        tt(T.Y2[:], T.XW[:, 0:4608].indirect(U("ZL")), T.XCB[:], A.add, XWK + " XWB ZL XCB", "Y2")
         pe([mm(T.GB[:, 0:16], T.TW[:, r, :], T.Y2[:, r:256:16], r == 0, r == 15) for r in range(16)], "TW Y2", "pGB")
         tt(C("kz"), T.R[:, 17:288:18], C("kc"), A.subtract, "R kc", "kz")
         tt(C("k"), C("kz"), C("nm1"), A.min, "kz nm1", "k")
@@ -540,16 +620,17 @@ def rank_program(g, core, T, topo):
         if t < V - 1:
             pe([mm(T.SM[:, 17, :], M("ONB"), T.GOT[:], True, True),
                 mm(T.SM[:, 20:23, :], M(GR), T.OU[:, 3 * t:3 * t + 3, :], True, True)], "ONB GOT %s %s" % (GR, uk), "pSM")
-        ts(T.YB[:], T.Y2[:], 0.5, A.mult, -1536.0, A.add, "Y2", "YB")
+        pe([mm(T.D1[:, 0, :, :], ID, T.Y2[:], True, True)], "IDB Y2", "pD1")
+        act(T.YB[:], T.D1[:, 0, :, :], ACT.Identity, "pD1", "YB", scale=0.5, bias=-1536.0)
         cp(I("z1"), T.GB[:, 0:16], "pGB", "z1")
         ts(I("z2"), I("z1"), 15, A.bitwise_and, None, None, "z1", "z2")
         tt(C("z3"), I("z2"), C("IC16"), A.add, "z2 IC16", "z3")
         cp(U("SL"), C("z3"), "z3", "SL")
         cp(T.X[:].indirect(U("SL")), T.YB[:], "YB SL X Xh", "X")
         if t < V - 1:
-            op("v", lambda: g.vector.tensor_reduce(T.ACOL[:], T.SM[:, 17, :], AxisListType.X, A.add), "pSM", "ACOL")
-            cp(T.OS[:, 3 * t:3 * t + 3, :], T.SM[:, 20:23, :], "pSM", "OS%d" % t)
-            remote(T.OC[:, 3 * t + 3:3 * t + 6, :], T.OS[:, 3 * t:3 * t + 3, :], "ao%d" % (t + 1), "OS%d" % t)
+            op("s", lambda: g.scalar.activation(C("u2"), T.SM[:, 17, :], ACT.Identity, accum_out=T.ACOL[:]), "pSM", "ACOL u2")
+            act(T.OS[:, 3 * t:3 * t + 3, :], T.SM[:, 20:23, :], ACT.Identity, "pSM", "OS%d" % t)
+            remote(T.OC[:, 3 * t + 3:3 * t + 6, :], T.OS[:, 3 * t:3 * t + 3, :], "ao%d" % (t + 1), "OS%d" % t, "OC%d" % (t + 1))
             ts(I("fi"), C("IC37"), T.ACOL[:], A.add, float(613 * (t + 1)), A.add, "IC37 ACOL", "fi")
             ts(I("fj"), I("fi"), 4095, A.bitwise_and, None, None, "fi", "fj")
             tt(C("na"), C("p0"), oc("OU", t, 2), A.is_gt, "p0 " + uk, "na")
@@ -567,7 +648,6 @@ def rank_program(g, core, T, topo):
     lengths("OU", t, uk)
     cp(T.PK2[:, 16:32], C("n"), "n", "PK2")
     norm2(T.T5B[:], "T5B")
-    norm3()
     pe(spread(T.GB, 512, T.PK2[:], True), "TBC PK2", "pGB")
     pe([mm(T.TB[:, 0:256], ID, T.XS[:], True, False), mm(T.TB[:, 0:256], M("ROTD"), T.XL[:], False, True)], "IDB ROTD XS XL", "pTB")
     act(T.YM[:], T.GB[:], ACT.Identity, "pGB", "YM")
@@ -582,6 +662,11 @@ def rank_program(g, core, T, topo):
     pe([mm(T.TB[:, 0:256], T.ROT6[:], T.HF[:], True, True)], "ROT6 HF", "pTB")
     cp(T.YH[:], T.TB[:, 0:256], "pTB", "YH")
     dma("y", [(T.yh[:], T.YH[:])], "YH", "yh", "oh")
+    for t in range(1, V):
+        arrive("al%d" % t, "LT%d" % t)
+        arrive("ao%d" % t, "OC%d" % t)
+    for i in order():
+        emit(*prog[i])
     for s in sorted(cnt):
         if clk["g"].get(s, 0) < cnt[s]:
             g.wait_ge(T.sem[s], cnt[s])

@@ -26,7 +26,7 @@ _sb("DEAD", [128, 16, 18], "bfloat16")
 _sb("SCN", [128, 16, 16], "bfloat16")
 _sb("H HX TR MTI", [128, 256], "int32")
 _sb("W", [128, 4096], "float32")
-_sb("D3", [8, 32, 256], "float32", "dram")
+_sb("RV", [8, 32, 256], "float32", "dram")
 _sb("THH THL ONE", [128, 288], "bfloat16")
 _sb("VC R", [128, 288], "float32")
 _sb("MB", [128, 128 * len(_MB)], "bfloat16")
@@ -50,7 +50,7 @@ _sb("LT", [128, 272 * V], "uint16")
 _sb("SD", [128, 272 * V], "uint16")
 _sb("OC OU OS", [128, 3 * V, 16], "bfloat16")
 _sb("YM", [128, 512], "float32")
-_sb("D0 D1", [128, 4, 16, 16], "float32", "psum")
+_sb("D0 D1 D2 D3", [128, 2, 16, 16], "float32", "psum")
 _sb("E", [128, 288], "float32", "psum")
 _sb("GB TB", [128, 512], "float32", "psum")
 _sb("SM", [128, 32, 16], "float32", "psum")
@@ -60,13 +60,18 @@ SEMAPHORES = (["sv", "ss", "sp", "sg", "ls", "lx0", "lx1", "lh", "lt", "lm", "lw
               + ["al%d" % t for t in range(1, V)] + ["ao%d" % t for t in range(1, V)])
 BIGV = {"XW0": 1.4, "XW1": 1.4, "XW2": 1.4, "XW3": 1.4, "XC": 0.43, "Y2": 0.45, "D0B": 0.45, "HX": 0.45, "X": 0.75, "R": 0.3,
         "OH": 0.27, "OHD": 0.27, "L1": 0.27, "XS": 0.47, "XL": 0.27, "LT0": 0.27, "TO16": 0.18, "DEAD": 0.27, "H": 0.27, "HM": 0.27,
-        "XC2": 0.3, "TIND": 0.9, "TINM": 0.9, "TW": 0.9, "MT": 0.7, "MTB": 0.3, "MTI": 0.27, "ZO": 0.2}
+        "XC2": 0.3, "XCB": 0.26, "XWc": 0.43, "TIND": 0.9, "TINM": 0.9, "TW": 0.9, "MT": 0.7, "MTB": 0.3, "MTI": 0.27, "ZO": 0.2}
 BIGS = {"XW0": 1.4, "XW1": 1.4, "XW2": 1.4, "XW3": 1.4, "AB0": 0.95, "AB1": 0.95, "AB2": 0.95, "AB3": 0.95, "XC2": 0.6, "ABc": 0.3,
-        "XCB": 0.3, "UF": 0.3, "A0B": 0.3, "XWB": 0.3, "YB": 0.3, "DEAD": 0.3, "LGD": 0.2, "AI": 0.2, "XWc": 0.42, "THH": 0.32, "THL": 0.32, "YM": 0.5, "YTF": 0.3}
-TRIES = 400
+        "XCB": 0.3, "UF": 0.3, "A0B": 0.3, "XWB": 0.3, "YB": 0.3, "DEAD": 0.3, "LGD": 0.2, "AI": 0.2, "XWc": 0.42, "THH": 0.32, "THL": 0.32, "YM": 0.5, "YTF": 0.3, "TINM": 1.8}
+TRIES = 60
+CLIMB = 3500
 CHOSEN = {}
 LOG = []
-PS = {"pD0", "pD1", "pE", "pGB", "pTB", "pSM"}
+VPIECES = (2, 5, 7)
+for _p in range(8):
+    BIGV["XW%d" % _p] = BIGS["XW%d" % _p] = 0.75
+    BIGS["AB%d" % _p] = 0.54
+PS = {"pD0", "pD1", "pD2", "pD3", "pE", "pGB", "pTB", "pSM"}
 
 
 def rank_program(g, core, T, topo):
@@ -117,7 +122,7 @@ def rank_program(g, core, T, topo):
             lastw[k] = (s, v)
             acc[k] = {s: v} if k in PS else {}
 
-    prog = []
+    prog, wide = [], {}
 
     def op(q, fns, R, W):
         prog.append((q, "c", fns if isinstance(fns, list) else [fns], R.split(), W.split(), own[q]))
@@ -145,11 +150,11 @@ def rank_program(g, core, T, topo):
         if kind == "d":
             return 0.1 * len(fns), 6.0 if w in ("X", "Xh") else 2.5
         if q == "p":
-            return 0.03 * len(fns), 0.08
+            return 0.028 * len(fns), 0.17
         if q == "g":
             return 0.8, 0.1
         big = BIGS if q == "s" else BIGV
-        return 0.1 + (big.get(w, 0.15 if q == "s" else 0.1) if len(fns) < 3 else 0.09 * len(fns)), 0.06
+        return (big.get(w, 0.13 if q == "s" else 0.11) if len(fns) < 3 else 0.09 * len(fns)) - 0.05, 0.17
 
     def order():
         n = len(prog)
@@ -158,6 +163,7 @@ def rank_program(g, core, T, topo):
         succ, npred = [[] for _ in range(n)], [0] * n
         lw, rd, ps = {}, {}, {}
         dur = [guess(p[0], p[1], p[2], p[4]) for p in prog]
+        dur = [(d[0] + wide.get(i, 0.0), d[1]) for i, d in enumerate(dur)]
         for i, (q, kind, fns, R, W, s) in enumerate(prog):
             pre = set()
             for k in R:
@@ -214,6 +220,20 @@ def rank_program(g, core, T, topo):
             got = play([float(tail[i] - a * i + noise[i]) for i in range(n)])
             if best is None or got[0] < best[0]:
                 best = got + (k, a)
+                key = [float(tail[i] - a * i + noise[i]) for i in range(n)]
+        rng = np.random.default_rng(1)
+        for k in range(CLIMB):
+            new = list(key)
+            if k % 2:
+                lo = int(rng.integers(0, n))
+                for i in range(lo, min(n, lo + 40)):
+                    new[i] += float(rng.normal(0.0, 2.0))
+            else:
+                for i in rng.integers(0, n, 12):
+                    new[int(i)] += float(rng.normal(0.0, 4.0))
+            got = play(new)
+            if got[0] <= best[0]:
+                best, key = got + (k, 0.0), new
         LOG.append(best[2:] + best[:1])
         CHOSEN[n] = best[1]
         return best[1]
@@ -241,7 +261,8 @@ def rank_program(g, core, T, topo):
     def mm(o, l, r, st, sp):
         return lambda: g.tensor.matmul(o, l, r, st, sp)
 
-    def pe(ms, R, W):
+    def pe(ms, R, W, more=0.0):
+        wide[len(prog)] = more
         op("p", ms, R, W)
 
     def fill(ap, c, W):
@@ -330,8 +351,9 @@ def rank_program(g, core, T, topo):
     ts(I("fj"), I("fi"), 4095, A.bitwise_and, None, None, "fi", "fj")
 
     def c_tail():
-        tt(C("d"), I("fj"), C("q"), A.subtract, "fj q", "d")
-        tt(C("d"), C("d"), C("na"), A.mult, "d na", "d")
+        tt(C("t9"), C("q"), C("na"), A.mult, "q na", "t9")
+        tt(C("q"), C("q"), C("t9"), A.subtract, "q t9", "q")
+        tt(C("d"), I("fj"), C("na"), A.mult, "fj na", "d")
         tt(C("cf"), C("q"), C("d"), A.add, "q d", "cf")
         cp(U("CL"), C("cf"), "cf", "CL")
 
@@ -345,12 +367,12 @@ def rank_program(g, core, T, topo):
         fill(T.OC[:, 1, :], 0.0, "OC0")
         fill(T.OC[:, 2, :], 1.0, "OC0")
         ts(T.CP[:, 3, :], T.CP[:, 3, :], 1.0, A.add, None, None, "CP", "CP")
-        ts(NI, ID, -1.0, A.mult, None, None, "IDB", "NIB")
-        ts(M("SCI"), ID, 8192.0, A.mult, None, None, "IDB", "SCI")
-        ts(M("PENI"), ID, -134217728.0, A.mult, None, None, "IDB", "PENI")
+        act(NI, ID, ACT.Identity, "IDB", "NIB", scale=-1.0)
+        act(M("SCI"), ID, ACT.Identity, "IDB", "SCI", scale=8192.0)
+        act(M("PENI"), ID, ACT.Identity, "IDB", "PENI", scale=-134217728.0)
+        act(T.TINM[:], T.TIND[:], ACT.Identity, "TIND", "TINM", scale=-8192.0)
 
     def setup_b():
-        ts(T.TINM[:], T.TIND[:], -8192.0, A.mult, None, None, "TIND", "TINM")
         ts(T.XS[:], T.TR[:], -2048.0, A.add, None, None, "TR", "XS")
         fill(T.XW[:, 4352:4624], 0.0, "XWc XWz")
         ts(C("DD"), C("IC"), -1.0, A.mult, 256.0, A.add, "IC", "DD")
@@ -400,32 +422,31 @@ def rank_program(g, core, T, topo):
         act(T.THL[:], T.E[:], ACT.Identity, "pE", "THL")
         fill(T.THH[:, 0:288:18], 4080.0, "THH")
 
-    XWK = "XW0 XW1 XW2 XW3 XWc"
+    XWK = "XW0 XW1 XW2 XW3 XW4 XW5 XW6 XW7 XWc"
 
-    def gather(q, t, b):
-        w = T.X[:].indirect(T.LT[:, 272 * t + 64 * b:272 * t + 64 * b + 64])
-        o = T.XW[:, 256 + 1024 * b:1280 + 1024 * b]
-        if q == "s":
-            act(o, w, ACT.Identity, XALL + " LT%d" % t, "XW%d" % b)
-        else:
-            cp(o, w, XALL + " LT%d" % t, "XW%d" % b)
+    def gather(t, b):
+        for p in (2 * b, 2 * b + 1):
+            w = T.X[:].indirect(T.LT[:, 272 * t + 32 * p:272 * t + 32 * p + 32])
+            o = T.XW[:, 256 + 512 * p:768 + 512 * p]
+            if p in VPIECES:
+                cp(o, w, XALL + " LT%d" % t, "XW%d" % p)
+            else:
+                act(o, w, ACT.Identity, XALL + " LT%d" % t, "XW%d" % p)
 
     def diff(b):
-        D = T["D%d" % (b % 2)]
-        ms = []
-        for h in range(2):
-            ms.append(mm(D[:, 2 * h:2 * h + 2, :, :], ID, T.XW[:, 256 + 1024 * b + 512 * h:768 + 1024 * b + 512 * h], True, False))
-            for s in range(8):
-                ms.append(mm(D[:, 2 * h:2 * h + 2, :, 2 * s:2 * s + 2], NI,
-                             T.XC2[:, 4 * b + 2 * h:4 * b + 2 * h + 2, :, :], False, s == 7))
-        pe(ms, "IDB NIB XC2 XW%d" % b, "pD%d" % (b % 2))
+        for p in (2 * b, 2 * b + 1):
+            D, k = T["D%d" % (p % 4)], "pD%d" % (p % 4)
+            pe([mm(D[:], ID, T.XW[:, 256 + 512 * p:768 + 512 * p], True, False)]
+               + [mm(D[:, :, :, 2 * s:2 * s + 2], NI, T.XC2[:, 2 * p:2 * p + 2, :, :], False, s == 7) for s in range(8)],
+               "IDB NIB XC2 XW%d" % p, k, 0.18)
 
     def absd(b):
-        act(T.AB[:, 4 * b:4 * b + 4, :, 1:17], T["D%d" % (b % 2)][:], ACT.Abs, "pD%d" % (b % 2), "AB%d" % b)
+        for p in (2 * b, 2 * b + 1):
+            act(T.AB[:, 2 * p:2 * p + 2, :, 1:17], T["D%d" % (p % 4)][:], ACT.Abs, "pD%d" % (p % 4), "AB%d" % p)
 
     def dsum(b, last=False):
         pe([mm(T.E[:, 72 * b:72 * b + 72], T.TINM[:, r, :], T.AB[:, 4 * b:4 * b + 4, r, :], False, last and r == 15)
-            for r in range(16)], "TINM ABz ABc AB%d" % b, "pE")
+            for r in range(16)], "TINM ABz ABc AB%d AB%d" % (2 * b, 2 * b + 1), "pE")
 
     def spread(dst, wid, src, first, last=True):
         return [mm(dst[:, r:wid:16], T.TBC[:, r, :], src, first, first or (last and r == 15)) for r in range(16)]
@@ -462,8 +483,8 @@ def rank_program(g, core, T, topo):
     def hand_pe(t):
         pe([mm(T.TB[:, 0:256], NI, T.XS[:], True, False)] + spread(T.TB, 256, T.c16[:], False, t == 0)
            + ([mm(T.TB[:, 0:256], M("ROTN"), T.XL[:], False, True)] if t else []),
-           "NIB TBC XS c16" + (" XL ROTN" if t else ""), "pTB")
-        pe([mm(T.GB[:], M("LGD"), T.ZO[:], True, False)] + spread(T.GB, 512, T.PK2[:], False), "LGD ZO TBC PK2", "pGB")
+           "NIB TBC XS c16" + (" XL ROTN" if t else ""), "pTB", 0.16)
+        pe([mm(T.GB[:], M("LGD"), T.ZO[:], True, False)] + spread(T.GB, 512, T.PK2[:], False), "LGD ZO TBC PK2", "pGB", 0.18)
 
     def hand_v():
         ts(T.OH[:], T.GB[:, 0:256], T.PM[:], A.is_equal, None, None, "pGB PM", "OH")
@@ -475,12 +496,29 @@ def rank_program(g, core, T, topo):
         if t > 0:
             ms.append(mm(T.TB[:, 0:256], M("REVD"), T.XL[:], False, False))
         ms.append(mm(T.TB[:, 0:256], T.REV32[:], T.OHD[:], False, True))
-        pe(ms, "REV REV32 XS OHD" + (" XL REVD" if t else ""), "pTB")
+        pe(ms, "REV REV32 XS OHD" + (" XL REVD" if t else ""), "pTB", 0.57)
 
     def hand_dma(t):
         act(T.UF[:], T.TB[:, 0:256], ACT.Identity, "pTB", "UF", bias=2048.0)
-        dma("y", [(T.D3[:, 0:16, :], T.UF[:]), (T.D3[:, 16:32, :], T.UF[:])], "UF", "D3", "hw%d" % t)
-        dma("y", [(T.W[:, 256 * e:256 * e + 256], T.D3[:, 15 - e:31 - e, :]) for e in range(16)], "D3", "W", "hr%d" % t)
+        dma("y", [(T.RV[:, 0:16, :], T.UF[:]), (T.RV[:, 16:32, :], T.UF[:])], "UF", "RV", "hw%d" % t)
+        dma("y", [(T.W[:, 256 * e:256 * e + 256], T.RV[:, 15 - e:31 - e, :]) for e in range(16)], "RV", "W", "hr%d" % t)
+
+    def hand_rest(t):
+        act(C("n16"), C("nm1"), ACT.Relu, "nm1", "n16", bias=-14.0)
+        act(C("t8"), C("n16"), ACT.Identity, "n16", "t8", scale=-16.0, bias=1.0)
+        tt(T.PK2[:, 0:16], C("t8"), C("nm1"), A.add, "t8 nm1", "PK2")
+        act(T.PK2[:, 16:32], C("m1"), ACT.Identity, "m1", "PK2", scale=8192.0)
+        act(M("LGD"), M("IDB"), ACT.Identity, "IDB LGS", "LGD", scale=T.LGS[:, t:t + 1])
+        if t > 0:
+            merge()
+        if t < V - 1:
+            ts(T.HM[:], T.H[:], -2048.0, A.add, RM(t + 1), A.mult, "H RM", "HM")
+            pe([mm(T.SM[:, 16, :], T.TIND[:, r, :], T.HM[:, r:256:16], r == 0, r == 15) for r in range(16)], "TIND HM", "pSM")
+        tt(C("t4"), C("m1"), C("nm1"), A.add, "m1 nm1", "t4")
+        act(C("t4"), C("t4"), ACT.Identity, "t4", "t4", scale=256.0, bias=256.0 * (t + 2))
+        tt(I("e1"), C("t4"), C("IC"), A.add, "t4 IC", "e1")
+        ts(I("e2"), I("e1"), 4095, A.bitwise_and, None, None, "e1", "e2")
+        cp(U("EL"), I("e2"), "e2", "EL")
 
     for t in range(V):
         ok, uk = "OC%d" % t, "OU%d" % t
@@ -489,7 +527,7 @@ def rank_program(g, core, T, topo):
         lt = T.LT[:, 272 * t:272 * t + 272]
         if t > 0:
             hand_pe(t - 1)
-        gather("s", t, 0)
+        gather(t, 0)
         c_tail()
         cp(T.XC[:], T.X[:].indirect(U("CL")), XALL + " CL", "XC")
         if t == 0:
@@ -498,8 +536,8 @@ def rank_program(g, core, T, topo):
         op("v", [(lambda e=e: g.vector.tensor_copy(T.XC2[:, :, :, e], T.XC[:])) for e in range(2)], "XC", "XC2")
         if t > 0:
             hand_v()
-        gather("v", t, 1)
-        gather("s", t, 2)
+        gather(t, 1)
+        gather(t, 2)
         diff(0)
         if t > 0:
             hand_u(t - 1)
@@ -511,8 +549,8 @@ def rank_program(g, core, T, topo):
             setup_b()
         else:
             hand_dma(t - 1)
-            act(T.XW[:, 4352:4608], T.X[:].indirect(T.LT[:, 272 * t + 256:272 * t + 272]), ACT.Identity, XALL + " " + ltk, "XWc")
-        gather("s", t, 3)
+            cp(T.XW[:, 4352:4608], T.X[:].indirect(T.LT[:, 272 * t + 256:272 * t + 272]), XALL + " " + ltk, "XWc")
+        gather(t, 3)
         if t > 0:
             cp(T.AINT[:], T.ACOL[:], "ACOL", "AINT")
             ts(T.AIN2[:], T.AINT[:], 255, A.bitwise_and, None, None, "AINT", "AIN2")
@@ -521,21 +559,21 @@ def rank_program(g, core, T, topo):
         ms = [mm(T.E[:], M("SCI"), T.THH[:], True, False), mm(T.E[:], M("SCI"), T.THL[:], False, False)]
         if t > 0:
             ms.append(mm(T.E[:], M("AI"), T.ONE[:], False, False))
-        pe(ms, "SCI THH THL" + (" AI ONE" if t else ""), "pE")
+        pe(ms, "SCI THH THL" + (" AI ONE" if t else ""), "pE", 0.28)
         if t > 0:
             ts(T.TO16[:], lt, -2048.0, A.add, None, None, ltk, "TO16")
             lengths("OC", t, ok)
             norm_compact("OC", t, ok)
             norm1(T.TO16[:, 0:256], T.TO16[:, 256:272], "TO16")
             pe([mm(T.SM[:, 0:16, :], ID, T.XW[:, 4352:4608], True, False), mm(T.SM[:, 0:16, :], NI, T.XC[:], False, True)],
-               "IDB NIB XWc XC", "pSM")
+               "IDB NIB XWc XC", "pSM", 0.16)
             act(T.AB[:, :, :, 17], T.SM[:, 0:16, :], ACT.Abs, "pSM", "ABc")
         absd(0)
         diff(1)
-        act(T.XCB[:], T.XC[:], ACT.Identity, "XC", "XCB", bias=3071.5)
+        ts(T.XCB[:], T.XC[:], 3071.5, A.add, None, None, "XC", "XCB")
         absd(1)
         pe([mm(T.SM[:, 0:16, :], ID, T.SCN[:], True, False)] + [mm(T.SM[:, 0:16, s], NI, hi, False, s == 15) for s in range(16)],
-           "IDB NIB SCN " + ok, "pSM")
+           "IDB NIB SCN " + ok, "pSM", 0.08)
         diff(2)
         if t == 0:
             lengths("OC", t, ok)
@@ -549,16 +587,16 @@ def rank_program(g, core, T, topo):
             if t > 0:
                 ms.append(mm(T.TB[:, 0:256], M(GRR), T.XL[:], False, True))
             ms.append(mm(T.TB[:, 256:272], M(GR), T.c16[:], True, True))
-            pe(ms, "%s XS c16" % GR + (" XL " + GRR if t else ""), "pTB")
+            pe(ms, "%s XS c16" % GR + (" XL " + GRR if t else ""), "pTB", 0.17)
         else:
             pe([mm(T.TB[:, 0:256], ID, T.XS[:], True, False), mm(T.TB[:, 0:256], M("ROTD"), T.XL[:], False, True)],
                "IDB ROTD XS XL", "pTB")
-        act(T.DEAD[:, :, 1:17], T.SM[:, 0:16, :], ACT.Relu, "pSM", "DEAD")
+        ts(T.DEAD[:, :, 1:17], T.SM[:, 0:16, :], 0.0, A.max, None, None, "pSM", "DEAD")
         if t == 0:
             setup_c()
         dsum(1)
         pe([mm(T.E[:], M("PENI"), T.DEAD[:], False, False), mm(T.E[:, 1:288:18], M("PENI"), lo, False, False),
-            mm(T.E[:, 17:288:18], M("PENI"), hit, False, False)], "PENI DEAD " + ok, "pE")
+            mm(T.E[:, 17:288:18], M("PENI"), hit, False, False)], "PENI DEAD " + ok, "pE", 0.1)
         absd(2)
         if t < V - 1:
             ts(T.SD[:, 272 * t:272 * t + 272], T.TB[:, 0:272], 2048.0, A.add, None, None, "pTB", "SD%d" % t)
@@ -566,7 +604,14 @@ def rank_program(g, core, T, topo):
         else:
             cp(T.T5B[:], T.TB[:, 0:256], "pTB", "T5B")
         diff(3)
+        if t == V - 1:
+            hand_rest(t)
+            hand_pe(t)
+            hand_v()
+            hand_u(t)
+            hand_dma(t)
         tt(C("kc"), C("KCB"), lo, A.add, "KCB " + ok, "kc")
+        tt(C("k"), C("kc"), C("n"), A.add, "kc n", "k")
         tt(C("b0"), C("DD"), hit, A.mult, "DD " + ok, "b0")
         tt(C("b0"), C("b0"), C("DN"), A.add, "b0 DN", "b0")
         ts(C("t2"), hi, 0.0, A.is_le, None, None, ok, "t2")
@@ -577,49 +622,31 @@ def rank_program(g, core, T, topo):
         absd(3)
         dsum(2)
         act(T.A0B[:], T.D0B[:], ACT.Abs, "D0B", "A0B", scale=2.0)
-        pe([mm(T.D0[:, 0, :, :], ID, T.A0B[:], True, False), mm(T.D0[:, 0, :, :], NI, T.XC[:], False, True)], "IDB NIB A0B XC", "pD0")
+        pe([mm(T.D0[:, 0, :, :], ID, T.A0B[:], True, False), mm(T.D0[:, 0, :, :], NI, T.XC[:], False, True)], "IDB NIB A0B XC", "pD0", 0.16)
         act(T.XW[:, 0:256], T.D0[:, 0, :, :], ACT.Identity, "pD0", "XWB", bias=0.5)
-        act(C("n16"), C("nm1"), ACT.Relu, "nm1", "n16", bias=-14.0)
-        act(C("t8"), C("n16"), ACT.Identity, "n16", "t8", scale=-16.0, bias=1.0)
-        tt(T.PK2[:, 0:16], C("t8"), C("nm1"), A.add, "t8 nm1", "PK2")
-        act(T.PK2[:, 16:32], C("m1"), ACT.Identity, "m1", "PK2", scale=8192.0)
-        act(M("LGD"), ID, ACT.Identity, "IDB LGS", "LGD", scale=T.LGS[:, t:t + 1])
-        if t > 0:
-            merge()
         if t < V - 1:
-            ts(T.HM[:], T.H[:], -2048.0, A.add, RM(t + 1), A.mult, "H RM", "HM")
-            pe([mm(T.SM[:, 16, :], T.TIND[:, r, :], T.HM[:, r:256:16], r == 0, r == 15) for r in range(16)], "TIND HM", "pSM")
-        tt(C("t4"), C("m1"), C("nm1"), A.add, "m1 nm1", "t4")
-        act(C("t4"), C("t4"), ACT.Identity, "t4", "t4", scale=256.0, bias=256.0 * (t + 2))
-        tt(I("e1"), C("t4"), C("IC"), A.add, "t4 IC", "e1")
-        ts(I("e2"), I("e1"), 4095, A.bitwise_and, None, None, "e1", "e2")
-        cp(U("EL"), I("e2"), "e2", "EL")
-        if t == V - 1:
-            hand_pe(t)
-            hand_v()
+            hand_rest(t)
         dsum(3, True)
         if t < V - 1:
             tt(C("q"), T.SM[:, 16, :], T.c16[:], A.subtract, "pSM c16", "q")
             act(C("u1"), C("p0"), ACT.Identity, "p0", "u1", scale=-1.0, bias=1.0)
             tt(C("q"), C("q"), C("u1"), A.mult, "q u1", "q")
             tt(C("q"), C("q"), C("cf"), A.add, "q cf", "q")
-        else:
-            hand_u(t)
-            hand_dma(t)
         op("v", lambda: g.vector.tensor_tensor_scan(T.R[:], T.E[:], T.VC[:], 0.0, A.max, A.min), "pE VC", "R")
         cp(U("ZL"), T.R[:, 17:288:18], "R", "ZL")
         tt(T.Y2[:], T.XW[:, 0:4608].indirect(U("ZL")), T.XCB[:], A.add, XWK + " XWB ZL XCB", "Y2")
         pe([mm(T.GB[:, 0:16], T.TW[:, r, :], T.Y2[:, r:256:16], r == 0, r == 15) for r in range(16)], "TW Y2", "pGB")
-        tt(C("kz"), T.R[:, 17:288:18], C("kc"), A.subtract, "R kc", "kz")
-        tt(C("k"), C("kz"), C("nm1"), A.min, "kz nm1", "k")
-        ts(oc("OU", t, 2), C("kz"), 0.0, A.is_ge, None, None, "kz", uk)
-        tt(C("g0"), C("n"), C("k"), A.subtract, "n k", "g0")
+        tt(C("kz"), C("k"), T.R[:, 17:288:18], A.subtract, "R k", "kz")
+        tt(oc("OU", t, 2), C("kz"), C("n"), A.is_le, "kz n", uk)
+        ts(C("g0"), C("kz"), 1.0, A.max, None, None, "kz", "g0")
         tt(T.GOT[:], C("g0"), oc("OU", t, 2), A.mult, "g0 " + uk, "GOT")
+        if t < V - 1:
+            pe([mm(T.SM[:, 17, :], M("ONB"), T.GOT[:], True, True)], "ONB GOT", "pSM")
+            op("s", lambda: g.scalar.activation(C("u2"), T.SM[:, 17, :], ACT.Identity, accum_out=T.ACOL[:]), "pSM", "ACOL u2")
         tt(oc("OU", t, 1), C("n16"), oc("OU", t, 2), A.is_gt, "n16 " + uk, uk)
         tt(oc("OU", t, 0), C("n"), T.GOT[:], A.subtract, "n GOT", uk)
         if t < V - 1:
-            pe([mm(T.SM[:, 17, :], M("ONB"), T.GOT[:], True, True),
-                mm(T.SM[:, 20:23, :], M(GR), T.OU[:, 3 * t:3 * t + 3, :], True, True)], "ONB GOT %s %s" % (GR, uk), "pSM")
+            pe([mm(T.SM[:, 20:23, :], M(GR), T.OU[:, 3 * t:3 * t + 3, :], True, True)], "%s %s" % (GR, uk), "pSM")
         pe([mm(T.D1[:, 0, :, :], ID, T.Y2[:], True, True)], "IDB Y2", "pD1")
         act(T.YB[:], T.D1[:, 0, :, :], ACT.Identity, "pD1", "YB", scale=0.5, bias=-1536.0)
         cp(I("z1"), T.GB[:, 0:16], "pGB", "z1")
@@ -628,7 +655,6 @@ def rank_program(g, core, T, topo):
         cp(U("SL"), C("z3"), "z3", "SL")
         cp(T.X[:].indirect(U("SL")), T.YB[:], "YB SL X Xh", "X")
         if t < V - 1:
-            op("s", lambda: g.scalar.activation(C("u2"), T.SM[:, 17, :], ACT.Identity, accum_out=T.ACOL[:]), "pSM", "ACOL u2")
             act(T.OS[:, 3 * t:3 * t + 3, :], T.SM[:, 20:23, :], ACT.Identity, "pSM", "OS%d" % t)
             remote(T.OC[:, 3 * t + 3:3 * t + 6, :], T.OS[:, 3 * t:3 * t + 3, :], "ao%d" % (t + 1), "OS%d" % t, "OC%d" % (t + 1))
             ts(I("fi"), C("IC37"), T.ACOL[:], A.add, float(613 * (t + 1)), A.add, "IC37 ACOL", "fi")

import numpy as np
from concourse.mybir import AluOpType, ActivationFunctionType

V = 6
SCRATCH = {}


def _sb(names, shape, dtype, where="sbuf"):
    for nm in names.split():
        SCRATCH[nm] = (where, shape, dtype)


_CF = ("m m1 q cf na d nm1 n kc t1 t2 t3 t4 kz k g0 n16 b0 z3 p0 u1 u2 t7 t8 t9 IC IC37 IC16 KCB DN DD ROW RM").split()
_CI = "fi fj z1 z2 e1 e2".split()
_CU = "CL ZL SL EL BL".split()
_MB = "IDB NIB SCI PENI GM REV ROTD REVD AI LGD ONB GR1 GR2 GRR1 GRR2 ZZB R6A R6B ROTN NI2".split()
_sb("X", [128, 4096], "bfloat16")
_sb("XW", [128, 4624], "bfloat16")
_sb("AB", [128, 16, 16, 18], "bfloat16")
_sb("XC D0B A0B YB OH", [128, 256], "bfloat16")
_sb("XC2", [128, 16, 16, 2], "bfloat16")
_sb("XCB OHD L1 UF HF YTF TSB YH YT", [128, 256], "float32")
_sb("Y2 XS XL HM T5B", [128, 256], "float16")
_sb("TO16", [128, 272], "float16")
_sb("DEAD", [128, 16, 18], "bfloat16")
_sb("SCN", [128, 16, 16], "bfloat16")
_sb("H HX TR MTI", [128, 256], "int32")
_sb("W", [128, 4096], "float32")
_sb("RV", [8, 32, 256], "float32", "dram")
_sb("THH THL ONE", [128, 288], "bfloat16")
_sb("VC R", [128, 288], "float32")
_sb("MB", [128, 128 * len(_MB)], "bfloat16")
_sb("ID32 REV32 ROT6 ONF", [128, 128], "float32")
_sb("TIND TINM TW TBC", [128, 16, 128], "bfloat16")
_sb("ZO", [128, 512], "bfloat16")
_sb("PI PMI WTI AINT AIN2", [128, 1], "int32")
_sb("PM WF ACOL AF PM16", [128, 1], "float32")
_sb("CF", [128, len(_CF), 16], "float32")
_sb("CI", [128, len(_CI), 16], "int32")
_sb("CU", [128, 16 * len(_CU)], "uint16")
_sb("LGI LGJ", [128, 8], "int32")
_sb("LGF LGS", [128, 8], "float32")
_sb("MT", [128, 768], "int32")
_sb("MTB", [128, 1024], "bfloat16")
_sb("CP", [128, 4, 16], "bfloat16")
_sb("c16", [128, 16], "float16")
_sb("GOT", [128, 16], "bfloat16")
_sb("PK1 PK2", [128, 32], "bfloat16")
_sb("LT", [128, 272 * V], "uint16")
_sb("SD", [128, 272 * V], "uint16")
_sb("OC OU OS", [128, 3 * V, 16], "bfloat16")
_sb("YM", [128, 512], "float32")
_sb("D0 D1 D2 D3", [128, 2, 16, 16], "float32", "psum")
_sb("E", [128, 288], "float32", "psum")
_sb("GB TB", [128, 512], "float32", "psum")
_sb("SM", [128, 32, 16], "float32", "psum")

SEMAPHORES = (["sv", "ss", "sp", "sg", "ls", "lx0", "lx1", "lh", "lt", "lm", "lw", "ox", "ox2", "oh", "oy", "om"]
              + ["hw%d" % t for t in range(V)] + ["hr%d" % t for t in range(V)]
              + ["al%d" % t for t in range(1, V)] + ["ao%d" % t for t in range(1, V)])
BIGV = {"XW0": 1.4, "XW1": 1.4, "XW2": 1.4, "XW3": 1.4, "XC": 0.43, "Y2": 0.45, "D0B": 0.45, "HX": 0.45, "X": 0.75, "R": 0.3,
        "OH": 0.27, "OHD": 0.27, "L1": 0.27, "XS": 0.47, "XL": 0.27, "LT0": 0.27, "TO16": 0.18, "DEAD": 0.27, "H": 0.27, "HM": 0.27,
        "XC2": 0.3, "XCB": 0.26, "XWc": 0.43, "TIND": 0.9, "TINM": 0.9, "TW": 0.9, "MT": 0.7, "MTB": 0.3, "MTI": 0.27, "ZO": 0.2}
BIGS = {"XW0": 1.4, "XW1": 1.4, "XW2": 1.4, "XW3": 1.4, "AB0": 0.95, "AB1": 0.95, "AB2": 0.95, "AB3": 0.95, "XC2": 0.6, "ABc": 0.3,
        "XCB": 0.3, "UF": 0.3, "A0B": 0.3, "XWB": 0.3, "YB": 0.3, "DEAD": 0.3, "LGD": 0.2, "AI": 0.2, "XWc": 0.42, "THH": 0.32, "THL": 0.32, "YM": 0.5, "YTF": 0.3, "TINM": 1.8}
TRIES = 60
CLIMB = 3500
CHOSEN = {}
LOG = []
VPIECES = (2, 5, 7)
for _p in range(8):
    BIGV["XW%d" % _p] = BIGS["XW%d" % _p] = 0.75
    BIGS["AB%d" % _p] = 0.54
PS = {"pD0", "pD1", "pD2", "pD3", "pE", "pGB", "pTB", "pSM"}


def rank_program(g, core, T, topo):
    rank = T.rank_of(core)
    if rank is None:
        return
    A = AluOpType
    ACT = ActivationFunctionType
    nxt = T.cores[(rank + 1) % len(T.cores)]
    neng = len(topo.engines(core, nxt))
    eng = {"v": g.vector, "s": g.scalar, "p": g.tensor, "g": g, "y": g.sync}
    own = {"v": "sv", "s": "ss", "p": "sp", "g": "sg"}
    cnt, tok, lastw, acc = {}, {}, {}, {}
    clk = {q: {} for q in eng}

    def need(q, R, W):
        nd = {}

        def add(t, mine):
            if t is None or (t[0] == own.get(q) and (q == "p" or not mine)):
                return
            if clk[q].get(t[0], 0) < t[1]:
                nd[t[0]] = max(nd.get(t[0], 0), t[1])
        for k in R:
            add(lastw.get(k), True)
            if k in PS:
                for t in acc.get(k, {}).items():
                    add(t, False)
        for k in W:
            add(lastw.get(k), True)
            for t in acc.get(k, {}).items():
                add(t, True)
        items = sorted(nd.items())
        for s, v in items:
            if clk[q].get(s, 0) >= v or any(tok.get(o, {}).get(s, 0) >= v for o in items if o[0] != s):
                continue
            eng[q].wait_ge(T.sem[s], v)
            clk[q][s] = v
            for s2, v2 in tok.get((s, v), {}).items():
                if clk[q].get(s2, 0) < v2:
                    clk[q][s2] = v2

    def done(q, s, v, R, W):
        tok[(s, v)] = dict(clk[q])
        for k in R:
            acc.setdefault(k, {})[s] = v
        for k in W:
            lastw[k] = (s, v)
            acc[k] = {s: v} if k in PS else {}

    prog, wide = [], {}

    def op(q, fns, R, W):
        prog.append((q, "c", fns if isinstance(fns, list) else [fns], R.split(), W.split(), own[q]))

    def dma(q, pairs, R, W, s):
        prog.append((q, "d", pairs, R.split(), W.split(), s))

    def emit(q, kind, fns, R, W, s):
        need(q, R, W if kind != "r" else [])
        if kind == "r":
            fns[0]()
            return
        for f in fns:
            if kind == "c":
                f().then_inc(T.sem[s], 1)
            else:
                eng[q].dma_start(f[0], f[1]).then_inc(T.sem[s], 16)
            cnt[s] = cnt.get(s, 0) + (1 if kind == "c" else 16)
        done(q, s, cnt[s], R, W)

    def guess(q, kind, fns, W):
        w = W[0]
        if kind == "r":
            return 1.0, 3.5
        if kind == "d":
            return 0.1 * len(fns), 6.0 if w in ("X", "Xh") else 2.5
        if q == "p":
            return 0.028 * len(fns), 0.17
        if q == "g":
            return 0.8, 0.1
        big = BIGS if q == "s" else BIGV
        return (big.get(w, 0.13 if q == "s" else 0.11) if len(fns) < 3 else 0.09 * len(fns)) - 0.05, 0.17

    def order():
        n = len(prog)
        if n in CHOSEN:
            return CHOSEN[n]
        succ, npred = [[] for _ in range(n)], [0] * n
        lw, rd, ps = {}, {}, {}
        dur = [guess(p[0], p[1], p[2], p[4]) for p in prog]
        dur = [(d[0] + wide.get(i, 0.0), d[1]) for i, d in enumerate(dur)]
        for i, (q, kind, fns, R, W, s) in enumerate(prog):
            pre = set()
            for k in R:
                if k in lw:
                    pre.add(lw[k])
            for k in W:
                if k in lw:
                    pre.add(lw[k])
                pre.update(rd.get(k, ()))
            for k in R + W:
                if k in PS:
                    pre.update(j for qq, j in ps.get(k, {}).items() if qq != q)
                    ps.setdefault(k, {})[q] = i
            for k in R:
                rd.setdefault(k, []).append(i)
            for k in W:
                lw[k], rd[k] = i, []
            pre.discard(i)
            for j in pre:
                succ[j].append(i)
            npred[i] = len(pre)
        tail = [0.0] * n
        for i in range(n - 1, -1, -1):
            tail[i] = dur[i][0] + max([dur[i][1] + tail[j] for j in succ[i]] or [0.0])

        def play(key):
            left = list(npred)
            ready = {q: [] for q in eng}
            at = [0.0] * n
            for i in range(n):
                if left[i] == 0:
                    ready[prog[i][0]].append(i)
            free = {q: 0.0 for q in eng}
            out, end = [], 0.0
            while len(out) < n:
                st, q = min((max(free[q], min(at[i] for i in ready[q])), q) for q in eng if ready[q])
                i = max([j for j in ready[q] if at[j] <= st + 0.02], key=lambda j: key[j])
                ready[q].remove(i)
                st = max(st, at[i])
                free[q] = st + dur[i][0]
                end = max(end, free[q] + dur[i][1])
                out.append(i)
                for j in succ[i]:
                    at[j] = max(at[j], free[q] + dur[i][1])
                    left[j] -= 1
                    if left[j] == 0:
                        ready[prog[j][0]].append(j)
            return end, out
        best = None
        for k in range(TRIES):
            rng = np.random.default_rng(k)
            a = float(rng.uniform(0.02, 0.3)) if k else 1.0
            noise = rng.normal(0.0, float(rng.uniform(0.0, 3.0)) if k else 0.0, n)
            got = play([float(tail[i] - a * i + noise[i]) for i in range(n)])
            if best is None or got[0] < best[0]:
                best = got + (k, a)
                key = [float(tail[i] - a * i + noise[i]) for i in range(n)]
        rng = np.random.default_rng(1)
        for k in range(CLIMB):
            new = list(key)
            if k % 2:
                lo = int(rng.integers(0, n))
                for i in range(lo, min(n, lo + 40)):
                    new[i] += float(rng.normal(0.0, 2.0))
            else:
                for i in rng.integers(0, n, 12):
                    new[int(i)] += float(rng.normal(0.0, 4.0))
            got = play(new)
            if got[0] <= best[0]:
                best, key = got + (k, 0.0), new
        LOG.append(best[2:] + best[:1])
        CHOSEN[n] = best[1]
        return best[1]

    def arrive(s, k):
        cnt[s] = neng
        tok[(s, neng)] = {}
        lastw[k] = (s, neng)

    def tt(o, a, b, f, R, W):
        op("v", lambda: g.vector.tensor_tensor(o, a, b, f), R, W)

    def ts(o, a, s1, f1, s2, f2, R, W):
        if f2 is None:
            op("v", lambda: g.vector.tensor_scalar(o, a, s1, None, f1), R, W)
        else:
            op("v", lambda: g.vector.tensor_scalar(o, a, s1, s2, f1, f2), R, W)

    def cp(o, a, R, W):
        op("v", lambda: g.vector.tensor_copy(o, a), R, W)

    def act(o, a, f, R, W, bias=0.0, scale=1.0):
        op("s", lambda: g.scalar.activation(o, a, f, bias=bias, scale=scale), R, W)

    def mm(o, l, r, st, sp):
        return lambda: g.tensor.matmul(o, l, r, st, sp)

    def pe(ms, R, W, more=0.0):
        wide[len(prog)] = more
        op("p", ms, R, W)

    def fill(ap, c, W):
        op("v", lambda: g.vector.memset(ap, c), "", W)

    def remote(dst, src, rs, key, lands):
        rid, pid, _ = topo.addr(nxt)
        prog.append(("g", "r", [lambda: g.remote_dma(dst, src, T.sem[rs], T.sem["ls"], pid, rid, topo.mask(core, nxt))],
                     [key], [lands], "ls"))
        cnt["ls"] = cnt.get("ls", 0) + neng

    def C(n):
        return T.CF[:, _CF.index(n), :]

    def I(n):
        return T.CI[:, _CI.index(n), :]

    def U(n):
        return T.CU[:, 16 * _CU.index(n):16 * _CU.index(n) + 16]

    def M(n, a=0, b=128, step=1):
        k = 128 * _MB.index(n)
        return T.MB[:, k + a:k + b:step]

    ID, NI = M("IDB"), M("NIB")
    XALL = "X Xh"

    dma("s", [(T.TR[:], T.trains[:])], "", "TR", "lt")
    dma("y", [(T.H[:], T.hands[:])], "", "H", "lh")
    fill(T.MT[:], 0, "MT")
    dma("s", [(T.X[:, 0:2048], T.x0[:, 0:2048])], "", "X", "lx0")
    dma("y", [(T.MT[0:128:16, 0:256], T.mh[:]), (T.MT[0:128:16, 256:512], T.nt[:]), (T.MT[0:128:16, 512:768], T.th[:])],
        "", "MT", "lm")
    dma("y", [(T.X[:, 2048:4096], T.x0[:, 2048:4096])], "", "Xh", "lx1")
    dma("y", [(T.WTI[:], T.wt[:])], "", "WTI", "lw")
    fill(M("ONB"), 1.0, "ONB")
    fill(T.ONF[:], 1.0, "ONF")
    fill(T.TIND[:], 0.0, "TIND")

    def iota(o, pat, base, cm, W, fl):
        if fl:
            op("g", lambda: g.iota(o, pat, base, cm, allow_small_or_imprecise_dtypes=True), "", W)
        else:
            op("g", lambda: g.iota(o, pat, base, cm), "", W)

    def pick(o, i, pat, c, b, m, R, W):
        op("g", lambda: g.affine_select(o, i, pat, c, 0.0, b, m), R, W)
    iota(T.PI[:], [[0, 1]], 0, 1, "PI", False)
    iota(C("ROW"), [[1, 16]], 0, 0, "ROW", True)
    pick(M("ZZB"), M("ONB"), [[-16, 8], [0, 16]], A.is_ge, 0, 1, "ONB", "ZZB")
    pick(M("GM"), M("ZZB"), [[16, 8], [0, 16]], A.is_ge, 15, -1, "ZZB", "GM")
    pick(ID, M("ONB"), [[-1, 128]], A.is_equal, 0, 1, "ONB", "IDB")
    iota(T.VC[:], [[256, 16], [1, 18]], 255, 0, "VC", True)
    iota(T.SCN[:], [[0, 16], [1, 16]], 1, 0, "SCN", True)
    iota(T.LGI[:], [[-1, 8]], 15, 1, "LGI", False)
    pick(M("REV"), M("ONB"), [[-16, 8], [1, 16]], A.is_equal, -15, 1, "ONB", "REV")
    pick(T.REV32[:], T.ONF[:], [[-16, 8], [1, 16]], A.is_equal, -15, 1, "ONF", "REV32")
    pick(T.ID32[:], T.ONF[:], [[-1, 128]], A.is_equal, 0, 1, "ONF", "ID32")
    pick(M("ROTD"), M("GM"), [[-16, 8], [-1, 16]], A.is_equal, -1, 1, "GM", "ROTD")
    pick(M("ZZB"), M("GM"), [[-16, 8], [-31, 16]], A.is_equal, 465, 1, "GM", "ZZB")
    pick(M("R6A"), M("GM"), [[-16, 8], [-1, 16]], A.is_equal, -6, 1, "GM", "R6A")
    pick(M("R6B"), M("GM"), [[-16, 8], [-1, 16]], A.is_equal, 10, 1, "GM", "R6B")
    pick(M("REVD"), M("GM"), [[-16, 8], [1, 16]], A.is_equal, -16, 1, "GM", "REVD")

    ts(T.PMI[:], T.PI[:], 15, A.bitwise_and, None, None, "PI", "PMI")
    cp(T.PM[:], T.PMI[:], "PMI", "PM")
    ts(C("RM"), C("ROW"), T.PM[:], A.is_equal, None, None, "ROW PM", "RM")
    ts(C("IC"), C("ROW"), 16.0, A.mult, T.PM[:], A.add, "ROW PM", "IC")
    RM = lambda k: T.CF[:, _CF.index("RM"), k:k + 1]
    op("v", [(lambda r=r: g.vector.tensor_copy(T.TIND[:, r, r:128:16], M("GM", r, 128, 16))) for r in range(16)], "GM TIND", "TIND")
    cp(T.LT[:, 0:256], T.TR[:], "TR", "LT0")
    ts(T.HM[:], T.H[:], -2048.0, A.add, RM(0), A.mult, "H RM", "HM")
    cp(T.MTB[:, 0:512], T.MT[:, 0:512], "MT", "MTB")
    ts(T.MTI[:], T.MT[:, 512:768], 4, A.arith_shift_right, None, None, "MT", "MTI")
    cp(T.MTB[:, 512:768], T.MTI[:], "MTI", "MTB")
    ts(T.MTI[:], T.MT[:, 512:768], 15, A.bitwise_and, None, None, "MT", "MTI")
    cp(T.MTB[:, 768:1024], T.MTI[:], "MTI", "MTB")
    pe([mm(T.SM[:, 20, :], T.TIND[:, r, :], T.HM[:, r:256:16], r == 0, r == 15) for r in range(16)], "TIND HM", "pSM")
    ts(C("q"), T.SM[:, 20, :], 2048.0, A.add, None, None, "pSM", "q")
    pe([mm(T.SM[:, 16:20, :], T.TIND[:, r, :], T.MTB[:, r:1024:16], r == 0, r == 15) for r in range(16)], "TIND MTB", "pSM")
    cp(T.CP[:], T.SM[:, 16:20, :], "pSM", "CP")
    cp(C("m"), T.CP[:, 0, :], "CP", "m")
    ts(C("na"), C("m"), 0.0, A.is_le, None, None, "m", "na")
    ts(C("IC37"), C("IC"), 37.0, A.mult, None, None, "IC", "IC37")
    cp(I("fi"), C("IC37"), "IC37", "fi")
    ts(I("fj"), I("fi"), 4095, A.bitwise_and, None, None, "fi", "fj")

    def c_tail():
        tt(C("t9"), C("q"), C("na"), A.mult, "q na", "t9")
        tt(C("q"), C("q"), C("t9"), A.subtract, "q t9", "q")
        tt(C("d"), I("fj"), C("na"), A.mult, "fj na", "d")
        tt(C("cf"), C("q"), C("d"), A.add, "q d", "cf")
        cp(U("CL"), C("cf"), "cf", "CL")

    def c_post():
        ts(T.c16[:], C("cf"), -2048.0, A.add, None, None, "cf", "c16")
        act(C("m1"), C("m"), ACT.Relu, "m", "m1", bias=-1.0)
        act(C("p0"), C("m1"), ACT.Relu, "m1", "p0", scale=-1.0, bias=1.0)

    def setup_a():
        cp(T.OC[:, 0, :], T.CP[:, 1, :], "CP", "OC0")
        fill(T.OC[:, 1, :], 0.0, "OC0")
        fill(T.OC[:, 2, :], 1.0, "OC0")
        ts(T.CP[:, 3, :], T.CP[:, 3, :], 1.0, A.add, None, None, "CP", "CP")
        act(NI, ID, ACT.Identity, "IDB", "NIB", scale=-1.0)
        act(M("SCI"), ID, ACT.Identity, "IDB", "SCI", scale=8192.0)
        act(M("PENI"), ID, ACT.Identity, "IDB", "PENI", scale=-134217728.0)
        act(T.TINM[:], T.TIND[:], ACT.Identity, "TIND", "TINM", scale=-8192.0)

    def setup_b():
        ts(T.XS[:], T.TR[:], -2048.0, A.add, None, None, "TR", "XS")
        fill(T.XW[:, 4352:4624], 0.0, "XWc XWz")
        ts(C("DD"), C("IC"), -1.0, A.mult, 256.0, A.add, "IC", "DD")
        fill(T.AB[:, :, :, 0], 0.0, "ABz")
        fill(T.AB[:, :, :, 17], 0.0, "ABc")
        for nm, j, src in (("GR1", 1, "IDB"), ("GR2", 2, "IDB")):
            cp(M(nm, 16 * j, 128), M(src, 0, 128 - 16 * j), src, nm)
            cp(M(nm, 0, 16 * j), M(src, 128 - 16 * j, 128), src, nm)
        ts(C("IC16"), C("IC"), 16.0, A.mult, None, None, "IC", "IC16")
        ts(C("KCB"), C("IC16"), 256.0, A.add, None, None, "IC16", "KCB")
        ts(C("DN"), C("IC"), -15.0, A.mult, 4096.0, A.add, "IC", "DN")
        ts(T.PM16[:], T.PM[:], 16.0, A.mult, None, None, "PM", "PM16")
        ts(T.VC[:], T.VC[:], T.PM16[:], A.add, None, None, "VC PM16", "VC")
        cp(T.VC[:, 0:288:18], C("IC"), "IC", "VC")
        ts(T.VC[:, 17:288:18], C("IC"), 4352.0, A.add, None, None, "IC", "VC")
        fill(T.DEAD[:], 0.0, "DEAD")

    def setup_c():
        cp(T.WF[:], T.WTI[:], "WTI", "WF")
        ts(T.WF[:], T.WF[:], 0.5, A.mult, None, None, "WF", "WF")
        ts(T.TW[:], T.TIND[:], T.WF[:], A.mult, None, None, "TIND WF", "TW")
        ts(T.LGJ[:], T.LGI[:], 15, A.bitwise_and, None, None, "LGI", "LGJ")
        cp(T.LGF[:], T.LGJ[:], "LGJ", "LGF")
        ts(T.LGS[:], T.LGF[:], -8192.0, A.mult, -4096.0, A.add, "LGF", "LGS")
        fill(T.ZO[:, 0:256], 0.0, "ZO")
        fill(T.ZO[:, 256:512], 1.0, "ZO")
        op("v", [(lambda r=r: g.vector.tensor_scalar(T.TBC[:, r, :], M("GM"), RM(r), None, A.mult)) for r in range(16)],
           "GM RM", "TBC")

    def setup_d():
        tt(M("ROTD"), M("ROTD"), M("ZZB"), A.add, "ROTD ZZB", "ROTD")
        tt(M("ROTD"), M("ROTD"), ID, A.subtract, "ROTD IDB", "ROTD")
        pick(M("ZZB"), M("GM"), [[-16, 8], [31, 16]], A.is_equal, 0, 1, "GM", "ZZB")
        ts(M("ROTN"), M("ROTD"), -1.0, A.mult, None, None, "ROTD", "ROTN")
        for nm, j, src in (("GRR1", 1, "ROTD"), ("GRR2", 2, "ROTD")):
            cp(M(nm, 16 * j, 128), M(src, 0, 128 - 16 * j), src, nm)
            cp(M(nm, 0, 16 * j), M(src, 128 - 16 * j, 128), src, nm)
        fill(T.ONE[:], 1.0, "ONE")
        tt(M("REVD"), M("REVD"), M("ZZB"), A.add, "REVD ZZB", "REVD")
        tt(M("REVD"), M("REVD"), M("REV"), A.subtract, "REVD REV", "REVD")
        tt(T.ROT6[:], M("R6A"), M("R6B"), A.add, "R6A R6B", "ROT6")

    def thresholds():
        pe([mm(T.E[:, k:288:18], ID, T.CP[:, 2, :], True, True) for k in range(18)], "IDB CP", "pE")
        act(T.THH[:], T.E[:], ACT.Identity, "pE", "THH", scale=16.0)
        pe([mm(T.E[:, k:288:18], ID, T.CP[:, 3, :], True, True) for k in range(18)], "IDB CP", "pE")
        act(T.THL[:], T.E[:], ACT.Identity, "pE", "THL")
        fill(T.THH[:, 0:288:18], 4080.0, "THH")

    XWK = "XW0 XW1 XW2 XW3 XW4 XW5 XW6 XW7 XWc"

    def gather(t, b):
        for p in (2 * b, 2 * b + 1):
            w = T.X[:].indirect(T.LT[:, 272 * t + 32 * p:272 * t + 32 * p + 32])
            o = T.XW[:, 256 + 512 * p:768 + 512 * p]
            if p in VPIECES:
                cp(o, w, XALL + " LT%d" % t, "XW%d" % p)
            else:
                act(o, w, ACT.Identity, XALL + " LT%d" % t, "XW%d" % p)

    def diff(b):
        for p in (2 * b, 2 * b + 1):
            D, k = T["D%d" % (p % 4)], "pD%d" % (p % 4)
            pe([mm(D[:], ID, T.XW[:, 256 + 512 * p:768 + 512 * p], True, False)]
               + [mm(D[:, :, :, 2 * s:2 * s + 2], NI, T.XC2[:, 2 * p:2 * p + 2, :, :], False, s == 7) for s in range(8)],
               "IDB NIB XC2 XW%d" % p, k, 0.18)

    def absd(b):
        for p in (2 * b, 2 * b + 1):
            act(T.AB[:, 2 * p:2 * p + 2, :, 1:17], T["D%d" % (p % 4)][:], ACT.Abs, "pD%d" % (p % 4), "AB%d" % p)

    def dsum(b, last=False):
        pe([mm(T.E[:, 72 * b:72 * b + 72], T.TINM[:, r, :], T.AB[:, 4 * b:4 * b + 4, r, :], False, last and r == 15)
            for r in range(16)], "TINM ABz ABc AB%d AB%d" % (2 * b, 2 * b + 1), "pE")

    def spread(dst, wid, src, first, last=True):
        return [mm(dst[:, r:wid:16], T.TBC[:, r, :], src, first, first or (last and r == 15)) for r in range(16)]

    def oc(b, t, k):
        return T[b][:, 3 * t + k, :]

    def norm_compact(b, t, key):
        act(T.PK1[:, 0:16], oc(b, t, 1), ACT.Identity, key, "PK1")
        act(C("t3"), oc(b, t, 2), ACT.Identity, key, "t3", scale=99.0)
        act(C("t7"), oc(b, t, 1), ACT.Identity, key, "t7", scale=-16.0)
        tt(C("t3"), C("t3"), oc(b, t, 0), A.add, "t3 " + key, "t3")
        tt(T.PK1[:, 16:32], C("t3"), C("t7"), A.add, "t3 t7", "PK1")

    def norm1(To, Cc, keys):
        pe([mm(T.TB[:, 0:256], NI, To, True, False)] + spread(T.TB, 256, Cc, False), "NIB TBC " + keys, "pTB")
        pe(spread(T.GB, 512, T.PK1[:], True), "TBC PK1", "pGB")

    def norm2(To, key):
        ts(T.OH[:], T.GB[:, 256:512], T.PM[:], A.is_equal, None, None, "pGB PM", "OH")
        tt(T.OHD[:], T.OH[:], T.TB[:, 0:256], A.mult, "OH pTB", "OHD")
        tt(T.XS[:], To, T.OHD[:], A.add, "OHD " + key, "XS")
        tt(T.XL[:], T.XS[:], T.GB[:, 0:256], A.mult, "XS pGB", "XL")

    def merge():
        tt(T.HX[:], T.W[:].indirect(U("EL")), T.L1[:], A.max, "W EL L1", "HX")
        ts(T.H[:], T.HX[:], 4095, A.bitwise_and, None, None, "HX", "H")

    def lengths(b, t, key):
        tt(C("nm1"), oc(b, t, 0), oc(b, t, 2), A.subtract, key, "nm1")
        tt(C("nm1"), C("nm1"), oc(b, t, 1), A.subtract, "nm1 " + key, "nm1")
        act(C("n"), C("nm1"), ACT.Identity, "nm1", "n", bias=1.0)

    def hand_pe(t):
        pe([mm(T.TB[:, 0:256], NI, T.XS[:], True, False)] + spread(T.TB, 256, T.c16[:], False, t == 0)
           + ([mm(T.TB[:, 0:256], M("ROTN"), T.XL[:], False, True)] if t else []),
           "NIB TBC XS c16" + (" XL ROTN" if t else ""), "pTB", 0.16)
        pe([mm(T.GB[:], M("LGD"), T.ZO[:], True, False)] + spread(T.GB, 512, T.PK2[:], False), "LGD ZO TBC PK2", "pGB", 0.18)

    def hand_v():
        ts(T.OH[:], T.GB[:, 0:256], T.PM[:], A.is_equal, None, None, "pGB PM", "OH")
        tt(T.OHD[:], T.OH[:], T.TB[:, 0:256], A.mult, "OH pTB", "OHD")
        tt(T.L1[:], T.H[:], T.GB[:, 256:512], A.add, "H pGB", "L1")

    def hand_u(t):
        ms = [mm(T.TB[:, 0:256], M("REV"), T.XS[:], True, False)]
        if t > 0:
            ms.append(mm(T.TB[:, 0:256], M("REVD"), T.XL[:], False, False))
        ms.append(mm(T.TB[:, 0:256], T.REV32[:], T.OHD[:], False, True))
        pe(ms, "REV REV32 XS OHD" + (" XL REVD" if t else ""), "pTB", 0.57)

    def hand_dma(t):
        act(T.UF[:], T.TB[:, 0:256], ACT.Identity, "pTB", "UF", bias=2048.0)
        dma("y", [(T.RV[:, 0:16, :], T.UF[:]), (T.RV[:, 16:32, :], T.UF[:])], "UF", "RV", "hw%d" % t)
        dma("y", [(T.W[:, 256 * e:256 * e + 256], T.RV[:, 15 - e:31 - e, :]) for e in range(16)], "RV", "W", "hr%d" % t)

    def hand_rest(t):
        act(C("n16"), C("nm1"), ACT.Relu, "nm1", "n16", bias=-14.0)
        act(C("t8"), C("n16"), ACT.Identity, "n16", "t8", scale=-16.0, bias=1.0)
        tt(T.PK2[:, 0:16], C("t8"), C("nm1"), A.add, "t8 nm1", "PK2")
        act(T.PK2[:, 16:32], C("m1"), ACT.Identity, "m1", "PK2", scale=8192.0)
        act(M("LGD"), M("IDB"), ACT.Identity, "IDB LGS", "LGD", scale=T.LGS[:, t:t + 1])
        if t > 0:
            merge()
        if t < V - 1:
            ts(T.HM[:], T.H[:], -2048.0, A.add, RM(t + 1), A.mult, "H RM", "HM")
            pe([mm(T.SM[:, 16, :], T.TIND[:, r, :], T.HM[:, r:256:16], r == 0, r == 15) for r in range(16)], "TIND HM", "pSM")
        tt(C("t4"), C("m1"), C("nm1"), A.add, "m1 nm1", "t4")
        act(C("t4"), C("t4"), ACT.Identity, "t4", "t4", scale=256.0, bias=256.0 * (t + 2))
        tt(I("e1"), C("t4"), C("IC"), A.add, "t4 IC", "e1")
        ts(I("e2"), I("e1"), 4095, A.bitwise_and, None, None, "e1", "e2")
        cp(U("EL"), I("e2"), "e2", "EL")

    for t in range(V):
        ok, uk = "OC%d" % t, "OU%d" % t
        ltk = "LT%d" % t
        hi, lo, hit = oc("OC", t, 0), oc("OC", t, 1), oc("OC", t, 2)
        lt = T.LT[:, 272 * t:272 * t + 272]
        if t > 0:
            hand_pe(t - 1)
        gather(t, 0)
        c_tail()
        cp(T.XC[:], T.X[:].indirect(U("CL")), XALL + " CL", "XC")
        if t == 0:
            setup_a()
            thresholds()
        op("v", [(lambda e=e: g.vector.tensor_copy(T.XC2[:, :, :, e], T.XC[:])) for e in range(2)], "XC", "XC2")
        if t > 0:
            hand_v()
        gather(t, 1)
        gather(t, 2)
        diff(0)
        if t > 0:
            hand_u(t - 1)
            tt(C("t1"), oc("OU", t - 1, 2), T.GOT[:], A.add, "GOT OU%d" % (t - 1), "t1")
            tt(C("t1"), C("m1"), C("t1"), A.add, "m1 t1", "t1")
            ts(C("m"), C("t1"), 16.0, A.min, None, None, "t1", "m")
        c_post()
        if t == 0:
            setup_b()
        else:
            hand_dma(t - 1)
            cp(T.XW[:, 4352:4608], T.X[:].indirect(T.LT[:, 272 * t + 256:272 * t + 272]), XALL + " " + ltk, "XWc")
        gather(t, 3)
        if t > 0:
            cp(T.AINT[:], T.ACOL[:], "ACOL", "AINT")
            ts(T.AIN2[:], T.AINT[:], 255, A.bitwise_and, None, None, "AINT", "AIN2")
            cp(T.AF[:], T.AIN2[:], "AIN2", "AF")
            act(M("AI"), M("SCI"), ACT.Identity, "SCI AF", "AI", scale=T.AF[:])
        ms = [mm(T.E[:], M("SCI"), T.THH[:], True, False), mm(T.E[:], M("SCI"), T.THL[:], False, False)]
        if t > 0:
            ms.append(mm(T.E[:], M("AI"), T.ONE[:], False, False))
        pe(ms, "SCI THH THL" + (" AI ONE" if t else ""), "pE", 0.28)
        if t > 0:
            ts(T.TO16[:], lt, -2048.0, A.add, None, None, ltk, "TO16")
            lengths("OC", t, ok)
            norm_compact("OC", t, ok)
            norm1(T.TO16[:, 0:256], T.TO16[:, 256:272], "TO16")
            pe([mm(T.SM[:, 0:16, :], ID, T.XW[:, 4352:4608], True, False), mm(T.SM[:, 0:16, :], NI, T.XC[:], False, True)],
               "IDB NIB XWc XC", "pSM", 0.16)
            act(T.AB[:, :, :, 17], T.SM[:, 0:16, :], ACT.Abs, "pSM", "ABc")
        absd(0)
        diff(1)
        ts(T.XCB[:], T.XC[:], 3071.5, A.add, None, None, "XC", "XCB")
        absd(1)
        pe([mm(T.SM[:, 0:16, :], ID, T.SCN[:], True, False)] + [mm(T.SM[:, 0:16, s], NI, hi, False, s == 15) for s in range(16)],
           "IDB NIB SCN " + ok, "pSM", 0.08)
        diff(2)
        if t == 0:
            lengths("OC", t, ok)
        else:
            norm2(T.TO16[:, 0:256], "TO16")
        dsum(0)
        j = 2 if (t + 1) % len(T.cores) == 0 else 1
        GR, GRR = "GR%d" % j, "GRR%d" % j
        if t < V - 1:
            ms = [mm(T.TB[:, 0:256], M(GR), T.XS[:], True, t == 0)]
            if t > 0:
                ms.append(mm(T.TB[:, 0:256], M(GRR), T.XL[:], False, True))
            ms.append(mm(T.TB[:, 256:272], M(GR), T.c16[:], True, True))
            pe(ms, "%s XS c16" % GR + (" XL " + GRR if t else ""), "pTB", 0.17)
        else:
            pe([mm(T.TB[:, 0:256], ID, T.XS[:], True, False), mm(T.TB[:, 0:256], M("ROTD"), T.XL[:], False, True)],
               "IDB ROTD XS XL", "pTB")
        ts(T.DEAD[:, :, 1:17], T.SM[:, 0:16, :], 0.0, A.max, None, None, "pSM", "DEAD")
        if t == 0:
            setup_c()
        dsum(1)
        pe([mm(T.E[:], M("PENI"), T.DEAD[:], False, False), mm(T.E[:, 1:288:18], M("PENI"), lo, False, False),
            mm(T.E[:, 17:288:18], M("PENI"), hit, False, False)], "PENI DEAD " + ok, "pE", 0.1)
        absd(2)
        if t < V - 1:
            ts(T.SD[:, 272 * t:272 * t + 272], T.TB[:, 0:272], 2048.0, A.add, None, None, "pTB", "SD%d" % t)
            remote(T.LT[:, 272 * t + 272:272 * t + 544], T.SD[:, 272 * t:272 * t + 272], "al%d" % (t + 1), "SD%d" % t, "LT%d" % (t + 1))
        else:
            cp(T.T5B[:], T.TB[:, 0:256], "pTB", "T5B")
        diff(3)
        if t == V - 1:
            hand_rest(t)
            hand_pe(t)
            hand_v()
            hand_u(t)
            hand_dma(t)
        tt(C("kc"), C("KCB"), lo, A.add, "KCB " + ok, "kc")
        tt(C("k"), C("kc"), C("n"), A.add, "kc n", "k")
        tt(C("b0"), C("DD"), hit, A.mult, "DD " + ok, "b0")
        tt(C("b0"), C("b0"), C("DN"), A.add, "b0 DN", "b0")
        ts(C("t2"), hi, 0.0, A.is_le, None, None, ok, "t2")
        tt(C("b0"), C("b0"), C("t2"), A.mult, "b0 t2", "b0")
        tt(C("b0"), C("b0"), C("kc"), A.add, "b0 kc", "b0")
        ts(U("BL"), C("b0"), -256.0, A.add, None, None, "b0", "BL")
        tt(T.D0B[:], T.XW[:, 256:4624].indirect(U("BL")), T.XC[:], A.subtract, XWK + " XWz BL XC", "D0B")
        absd(3)
        dsum(2)
        act(T.A0B[:], T.D0B[:], ACT.Abs, "D0B", "A0B", scale=2.0)
        pe([mm(T.D0[:, 0, :, :], ID, T.A0B[:], True, False), mm(T.D0[:, 0, :, :], NI, T.XC[:], False, True)], "IDB NIB A0B XC", "pD0", 0.16)
        act(T.XW[:, 0:256], T.D0[:, 0, :, :], ACT.Identity, "pD0", "XWB", bias=0.5)
        if t < V - 1:
            hand_rest(t)
        dsum(3, True)
        if t < V - 1:
            tt(C("q"), T.SM[:, 16, :], T.c16[:], A.subtract, "pSM c16", "q")
            act(C("u1"), C("p0"), ACT.Identity, "p0", "u1", scale=-1.0, bias=1.0)
            tt(C("q"), C("q"), C("u1"), A.mult, "q u1", "q")
            tt(C("q"), C("q"), C("cf"), A.add, "q cf", "q")
        op("v", lambda: g.vector.tensor_tensor_scan(T.R[:], T.E[:], T.VC[:], 0.0, A.max, A.min), "pE VC", "R")
        cp(U("ZL"), T.R[:, 17:288:18], "R", "ZL")
        tt(T.Y2[:], T.XW[:, 0:4608].indirect(U("ZL")), T.XCB[:], A.add, XWK + " XWB ZL XCB", "Y2")
        pe([mm(T.GB[:, 0:16], T.TW[:, r, :], T.Y2[:, r:256:16], r == 0, r == 15) for r in range(16)], "TW Y2", "pGB")
        tt(C("kz"), C("k"), T.R[:, 17:288:18], A.subtract, "R k", "kz")
        tt(oc("OU", t, 2), C("kz"), C("n"), A.is_le, "kz n", uk)
        ts(C("g0"), C("kz"), 1.0, A.max, None, None, "kz", "g0")
        tt(T.GOT[:], C("g0"), oc("OU", t, 2), A.mult, "g0 " + uk, "GOT")
        if t < V - 1:
            pe([mm(T.SM[:, 17, :], M("ONB"), T.GOT[:], True, True)], "ONB GOT", "pSM")
            op("s", lambda: g.scalar.activation(C("u2"), T.SM[:, 17, :], ACT.Identity, accum_out=T.ACOL[:]), "pSM", "ACOL u2")
        tt(oc("OU", t, 1), C("n16"), oc("OU", t, 2), A.is_gt, "n16 " + uk, uk)
        tt(oc("OU", t, 0), C("n"), T.GOT[:], A.subtract, "n GOT", uk)
        if t < V - 1:
            pe([mm(T.SM[:, 20:23, :], M(GR), T.OU[:, 3 * t:3 * t + 3, :], True, True)], "%s %s" % (GR, uk), "pSM")
        pe([mm(T.D1[:, 0, :, :], ID, T.Y2[:], True, True)], "IDB Y2", "pD1")
        act(T.YB[:], T.D1[:, 0, :, :], ACT.Identity, "pD1", "YB", scale=0.5, bias=-1536.0)
        cp(I("z1"), T.GB[:, 0:16], "pGB", "z1")
        ts(I("z2"), I("z1"), 15, A.bitwise_and, None, None, "z1", "z2")
        tt(C("z3"), I("z2"), C("IC16"), A.add, "z2 IC16", "z3")
        cp(U("SL"), C("z3"), "z3", "SL")
        cp(T.X[:].indirect(U("SL")), T.YB[:], "YB SL X Xh", "X")
        if t < V - 1:
            act(T.OS[:, 3 * t:3 * t + 3, :], T.SM[:, 20:23, :], ACT.Identity, "pSM", "OS%d" % t)
            remote(T.OC[:, 3 * t + 3:3 * t + 6, :], T.OS[:, 3 * t:3 * t + 3, :], "ao%d" % (t + 1), "OS%d" % t, "OC%d" % (t + 1))
            ts(I("fi"), C("IC37"), T.ACOL[:], A.add, float(613 * (t + 1)), A.add, "IC37 ACOL", "fi")
            ts(I("fj"), I("fi"), 4095, A.bitwise_and, None, None, "fi", "fj")
            tt(C("na"), C("p0"), oc("OU", t, 2), A.is_gt, "p0 " + uk, "na")
        if t == 0:
            setup_d()

    t, uk = V - 1, "OU%d" % (V - 1)
    dma("y", [(T.yx[:, 0:2048], T.X[:, 0:2048])], XALL, "yx", "ox")
    dma("s", [(T.yx[:, 2048:4096], T.X[:, 2048:4096])], XALL, "yx2", "ox2")
    tt(C("t1"), oc("OU", t, 2), T.GOT[:], A.add, "GOT " + uk, "t1")
    tt(C("t1"), C("m1"), C("t1"), A.add, "m1 t1", "t1")
    ts(T.PK2[:, 0:16], C("t1"), 16.0, A.min, None, None, "t1", "PK2")
    norm_compact("OU", t, uk)
    norm1(T.T5B[:], T.c16[:], "T5B c16")
    lengths("OU", t, uk)
    cp(T.PK2[:, 16:32], C("n"), "n", "PK2")
    norm2(T.T5B[:], "T5B")
    pe(spread(T.GB, 512, T.PK2[:], True), "TBC PK2", "pGB")
    pe([mm(T.TB[:, 0:256], ID, T.XS[:], True, False), mm(T.TB[:, 0:256], M("ROTD"), T.XL[:], False, True)], "IDB ROTD XS XL", "pTB")
    act(T.YM[:], T.GB[:], ACT.Identity, "pGB", "YM")
    dma("y", [(T.ym[:], T.YM[0:128:16, 0:256]), (T.yn[:], T.YM[0:128:16, 256:512])], "YM", "ym yn", "om")
    act(T.YTF[:], T.TB[:, 0:256], ACT.Identity, "pTB", "YTF", bias=2048.0)
    ts(T.TSB[:], T.YM[:, 256:512], T.PM[:], A.is_gt, None, None, "YM PM", "TSB")
    tt(T.YT[:], T.YTF[:], T.TSB[:], A.mult, "YTF TSB", "YT")
    dma("s", [(T.yt[:], T.YT[:])], "YT", "yt", "oy")
    ts(T.TSB[:], T.YM[:, 0:256], T.LGF[:, V - 1:V], A.is_gt, None, None, "YM LGF", "TSB")
    merge()
    tt(T.HF[:], T.H[:], T.TSB[:], A.mult, "H TSB", "HF")
    pe([mm(T.TB[:, 0:256], T.ROT6[:], T.HF[:], True, True)], "ROT6 HF", "pTB")
    cp(T.YH[:], T.TB[:, 0:256], "pTB", "YH")
    dma("y", [(T.yh[:], T.YH[:])], "YH", "yh", "oh")
    for t in range(1, V):
        arrive("al%d" % t, "LT%d" % t)
        arrive("ao%d" % t, "OC%d" % t)
    for i in order():
        emit(*prog[i])
    for s in sorted(cnt):
        if clk["g"].get(s, 0) < cnt[s]:
            g.wait_ge(T.sem[s], cnt[s])
